import numpy as np
import ml_dtypes


def mxq(x, axis, fmt="e4m3"):
    dtype, down = {"e4m3": (ml_dtypes.float8_e4m3fn, 7), "e5m2": (ml_dtypes.float8_e5m2, 14)}[fmt]
    v = np.moveaxis(np.asarray(x, np.float32).astype(ml_dtypes.bfloat16).astype(np.float64), axis, -1)
    blocks = v.reshape(v.shape[:-1] + (-1, 32))
    amax = np.abs(blocks).max(-1, keepdims=True)
    byte = np.maximum(np.where(amax > 0, np.frexp(amax)[1] - 1 + 127, 0) - down, 1)
    scale = np.exp2(byte - 127.0)
    codes = (blocks / scale).astype(np.float32).astype(dtype).astype(np.float64)
    return np.moveaxis((codes * scale).reshape(v.shape), -1, axis)


WIDE = False


def mx_kscale(k):
    if not WIDE:
        return np.ones(k)
    levels = np.array([10, -10, 5, -5, 0])
    if k % 512:
        return np.exp2(np.random.permutation(np.resize(levels, k // 32))).repeat(32)
    a = np.empty((k // 512, 16))
    for p in range(k // 512):
        a[p, :8] = np.random.permutation(np.resize(levels, 8))
        for g in range(8):
            far = levels[np.abs(levels - a[p, g]) >= 10]
            a[p, g + 8] = far[np.random.randint(len(far))]
    return np.exp2(a.ravel()).repeat(32)


BF16 = ml_dtypes.bfloat16


def bf(x):
    return np.asarray(x, np.float32).astype(BF16)


def f64(x):
    return np.asarray(x).astype(np.float64)


E2M1 = np.array([0.0, 0.5, 1.0, 1.5, 2.0, 3.0, 4.0, 6.0, -0.0, -0.5, -1.0, -1.5, -2.0, -3.0, -4.0, -6.0])


def pack_weight(w, fmt):
    k, n = w.shape
    w = f64(bf(w)).reshape(k // 32, 32, n)
    amax = np.abs(w).max(1)
    if fmt == "e4m3":
        byte = np.frexp(amax)[1] - 1 + 127 - 7
    else:
        mant, ex = np.frexp(amax / 6.0)
        byte = np.where(mant > 0.5, ex, ex - 1) + 127
    byte = np.clip(np.where(amax > 0, byte, 1), 1, 254)
    scaled = (w * np.exp2(127.0 - byte)[:, None, :]).reshape(k, n).astype(np.float32)
    by_word = np.ascontiguousarray(scaled.reshape(k // 512, 128, 4, n).transpose(0, 1, 3, 2))
    if fmt == "e4m3":
        words = by_word.astype(ml_dtypes.float8_e4m3fn).view(np.uint8)
    else:
        c = by_word.astype(ml_dtypes.float4_e2m1fn).view(np.uint8) & 0xF
        words = c[..., 0::2] | (c[..., 1::2] << 4)
    return np.ascontiguousarray(words), np.ascontiguousarray(byte.astype(np.uint8).reshape(k // 512, 16, n))


def unpack_weight(words, scales, fmt):
    g, p, n, _ = words.shape
    if fmt == "e4m3":
        vals = np.ascontiguousarray(words).view(ml_dtypes.float8_e4m3fn).astype(np.float64)
    else:
        nib = np.empty((g, p, n, 4), np.uint8)
        nib[..., 0::2] = words & 0xF
        nib[..., 1::2] = words >> 4
        vals = E2M1[nib]
    vals = vals * np.repeat(np.exp2(scales.astype(np.float64) - 127.0), 8, axis=1)[..., None]
    return vals.transpose(0, 1, 3, 2).reshape(g * 512, n)
def pack4(w):
    words, scales = pack_weight(w, "e2m1")
    return words.reshape(words.shape[0], 128, -1), scales


def unpack4(words, scales):
    return unpack_weight(words.reshape(words.shape[0], 128, -1, 2), scales, "e2m1")


M, K1, K2, F, B = 1024, 512, 1536, 1024, 2048


def draw0():
    s1, s2 = mx_kscale(K1), mx_kscale(K2)
    t = mx_kscale(F)
    code_new = np.random.standard_normal((M, K1)) / np.sqrt(K1 + K2)
    code_old = np.random.standard_normal((M, K2)) / np.sqrt(K1 + K2)
    a_new = np.random.standard_normal((K1, F))
    a_old = np.random.standard_normal((K2, F))
    x = np.random.standard_normal((F, B)) / np.sqrt(F)
    old_words, old_scales = pack4(a_old / s2[:, None])
    x_words, x_scales = pack4(x / t[:, None])
    return {"code_new": bf(code_new * s1),
            "data_new": bf(a_new / s1[:, None]),
            "code_old": bf(code_old * s2),
            "old_words": old_words,
            "old_scales": old_scales,
            "mask": bf(0.5 * np.random.standard_normal((M, F))),
            "feature_scale": bf((1 + 0.1 * np.random.standard_normal(F)) * t),
            "x_words": x_words,
            "x_scales": x_scales}


def core(code_new, data_new, code_old, old_words, old_scales, mask, feature_scale, x_words, x_scales):
    new = mxq(f64(code_new), 1, "e4m3") @ mxq(f64(data_new), 0, "e4m3")
    old = mxq(f64(code_old), 1, "e4m3") @ unpack4(old_words, old_scales)
    coded = (new + old + f64(mask)) * f64(feature_scale)
    y = mxq(coded, 1, "e4m3") @ unpack4(x_words, x_scales)
    return y


def e4m3fn_bytes(y):
    return np.clip(np.asarray(y, np.float64), -448.0, 448.0).astype(np.float32).astype(ml_dtypes.float8_e4m3fn).view(np.uint8)


def e4m3fn_values(b):
    return np.asarray(b, np.uint8).view(ml_dtypes.float8_e4m3fn).astype(np.float64)


def setup_inputs():
    d = draw0()
    x0 = np.asarray(d['code_old']).astype(np.float64)
    s = (np.max(np.abs(x0), axis=(0,), keepdims=True) / 448.0).astype(np.float32)
    out = {}
    for k, v in d.items():
        if k == 'code_old':
            out['code_old_bytes'] = e4m3fn_bytes(x0 / s.astype(np.float64))
            out['code_old_scale'] = s
        else:
            out[k] = v
    return out


def reference(code_new, data_new, code_old_bytes, code_old_scale, old_words, old_scales, mask, feature_scale, x_words, x_scales):
    return core(code_new, data_new, e4m3fn_values(code_old_bytes) * code_old_scale.astype(np.float64), old_words, old_scales, mask, feature_scale, x_words, x_scales)

@@ -1,0 +1,410 @@
+from contextlib import ExitStack
+
+import concourse.mybir as mybir
+from concourse.masks import make_identity
+
+M, K1, K2, F, B = 1024, 512, 1536, 1024, 2048
+FLOPS = 2 * M * (K1 + K2) * F + 2 * M * F * B
+
+F32 = mybir.dt.float32
+BF16 = mybir.dt.bfloat16
+I32 = mybir.dt.int32
+U32 = mybir.dt.uint32
+U8 = mybir.dt.uint8
+FP8 = mybir.dt.float8_e4m3fn
+FP8X4 = mybir.dt.float8_e4m3fn_x4
+FP4X4 = mybir.dt.float4_e2m1fn_x4
+ADD = mybir.AluOpType.add
+MULT = mybir.AluOpType.mult
+
+P = 128
+PACK = 4
+K_PASS = P * PACK
+NH = 512
+FP4_BYTES = 2
+
+TILES = M // P
+PAIRS = TILES // 2
+HALVES = F // NH
+OLD_PASSES = K2 // K_PASS
+PASSES = (K1 + K2) // K_PASS
+X_PASSES = F // K_PASS
+X_BLOCKS = B // NH
+
+
+def tile_coded_worker_products_s3_kernel(
+    tc, code_new, data_new, code_old_bytes, code_old_scale, old_words, old_scales, mask, feature_scale, x_words, x_scales, out
+):
+    nc = tc.nc
+    scalar_copy, vector_copy = nc.scalar.copy, nc.vector.tensor_copy
+
+    with ExitStack() as ctx:
+        keep = ctx.enter_context(tc.tile_pool(name="keep", bufs=1))
+        work = ctx.enter_context(tc.tile_pool(name="work", bufs=3))
+        psum = ctx.enter_context(tc.psum_pool(name="psum", bufs=1))
+        ctx.enter_context(tc.manual_schedule())
+
+        old_plane = keep.tile([P, OLD_PASSES, F], U8, align_bytes=64)
+        x_plane = keep.tile([P, X_PASSES, B], U8, align_bytes=64)
+        primer = keep.tile([P, 2], F32)
+        nc.vector.memset(primer[:], 0.0)
+        nc.vector.memset(old_plane[:].rearrange("p g n -> p (g n)").bitcast(I32), 0)
+        nc.vector.memset(x_plane[:].rearrange("p g n -> p (g n)").bitcast(I32), 0)
+
+        scale_cols = []
+        for g in range(OLD_PASSES):
+            cols = keep.tile([P, PACK], F32, name=f"scale_cols_{g}")
+            nc.scalar.dma_start(out=cols[:], in_=code_old_scale.rearrange("o (g p c) -> g p (o c)", p=P, c=PACK)[g])
+            scale_cols.append(cols)
+        feature_cols_f32 = keep.tile([P, HALVES, PACK], F32)
+        feature_cols = keep.tile([P, HALVES, PACK], BF16)
+        nc.scalar.dma_start(out=feature_cols[:], in_=feature_scale.rearrange("(g p c) -> p g c", p=P, c=PACK))
+        nc.scalar.copy(out=primer[:, 1:2], in_=primer[:, 0:1])
+        ident = keep.tile([P, P], F32)
+        make_identity(nc, ident[:])
+
+        old_rows = code_old_bytes.rearrange("(j p i) k -> j p i k", p=P, i=2)
+        new_rows = code_new.rearrange("(j p i) k -> j p i k", p=P, i=2)
+        mask_rows = mask.rearrange("(j p i) f -> j p i f", p=P, i=2)
+        out_rows = out.rearrange("(j p i) b -> j i p b", p=P, i=2)
+
+        old_bytes = []
+        code_rows = []
+        mask_tiles = []
+        for j in range(PAIRS):
+            ob = keep.tile([P, 2, K2], U8, name=f"old_bytes_{j}")
+            cr = keep.tile([P, 2, K1 + K2], BF16, name=f"code_rows_{j}", align_bytes=64)
+            mk = keep.tile([P, 2, F], BF16, name=f"mask_{j}")
+            old_bytes.append(ob)
+            code_rows.append(cr)
+            mask_tiles.append(mk)
+        data_raw = keep.tile([P, PACK, F], BF16)
+        old_code = []
+        for h in range(HALVES):
+            oc = keep.tile([P, OLD_PASSES, FP4_BYTES * NH], U8, name=f"old_code_{h}", align_bytes=64)
+            old_code.append(oc)
+        x_code = []
+        for g in range(X_PASSES):
+            xc = keep.tile([P, FP4_BYTES * B], U8, name=f"x_code_{g}", align_bytes=64)
+            x_code.append(xc)
+
+        def load_first_pair(i):
+            nc.sync.dma_start(out=old_bytes[0][:, i, :], in_=old_rows[0, :, i, :])
+            nc.sync.dma_start(out=code_rows[0][:, i, 0:K1], in_=new_rows[0, :, i, :])
+
+        def load_old_pair(j):
+            nc.sync.dma_start(out=old_bytes[j][:], in_=old_rows[j])
+
+        def load_new_pair(j):
+            nc.sync.dma_start(out=code_rows[j][:, :, 0:K1], in_=new_rows[j])
+
+        def load_mask(j):
+            nc.sync.dma_start(out=mask_tiles[j][:], in_=mask_rows[j])
+
+        def load_old_code(h):
+            cols = slice(FP4_BYTES * NH * h, FP4_BYTES * NH * (h + 1))
+            nc.sync.dma_start(out=old_code[h][:], in_=old_words.rearrange("g p n -> p g n")[:, :, cols])
+
+        def load_x_code(g):
+            nc.sync.dma_start(out=x_code[g][:], in_=x_words[g])
+
+        def load_scales(plane, source):
+            for q in range(4):
+                nc.sync.dma_start(
+                    out=plane[32 * q : 32 * q + 4, :, :].bitcast(I32),
+                    in_=source.rearrange("g q n -> q g n")[4 * q : 4 * q + 4, :, :].bitcast(I32),
+                )
+
+        load_first_pair(0)
+        nc.sync.dma_start(out=data_raw[:], in_=data_new.rearrange("(p t) f -> p t f", t=PACK))
+        load_first_pair(1)
+        load_old_pair(1)
+        load_scales(old_plane, old_scales)
+        load_new_pair(1)
+        load_old_code(0)
+        load_old_code(1)
+        load_mask(0)
+        load_x_code(0)
+        load_old_pair(2)
+        load_new_pair(2)
+        load_x_code(1)
+        load_scales(x_plane, x_scales)
+        load_mask(1)
+        load_old_pair(3)
+        load_new_pair(3)
+        load_mask(2)
+        load_mask(3)
+
+        scale_all = keep.tile([P, K2], F32)
+        feature_all = keep.tile([P, F], F32)
+
+        def spread(bank, cols):
+            for c in range(PACK):
+                nc.tensor.transpose(bank[:, c, :], cols[:, c : c + 1].to_broadcast([P, P]), ident[:])
+
+        def collect(dst, bank):
+            nc.scalar.copy(out=dst.rearrange("p (n c) -> p n c", c=PACK), in_=bank[:].rearrange("p c n -> p n c"))
+
+        scale_banks = []
+        for g in range(OLD_PASSES):
+            if g < 2:
+                bank = psum.tile([P, PACK, P], F32, name=f"scale_bank_{g}", tag="code_bank", bufs=2)
+            else:
+                bank = psum.tile([P, PACK, P], F32, name=f"scale_bank_{g}", tag="coded_bank", bufs=1)
+            spread(bank, scale_cols[g])
+            scale_banks.append(bank)
+        for g in range(OLD_PASSES):
+            collect(scale_all[:, K_PASS * g : K_PASS * (g + 1)], scale_banks[g])
+        nc.scalar.copy(out=feature_cols_f32[:], in_=feature_cols[:])
+
+        def spread_features(h):
+            bank = psum.tile([P, PACK, P], F32, name=f"feature_bank_{h}", tag="code_bank", bufs=2)
+            spread(bank, feature_cols_f32[:, h, :])
+            collect(feature_all[:, NH * h : NH * (h + 1)], bank)
+
+        data_grouped = []
+        data_codes = []
+        data_scales = []
+        for h in range(HALVES):
+            dg = keep.tile([P, NH, PACK], BF16, name=f"data_grouped_{h}", align_bytes=64)
+            dc = keep.tile([P, NH], U32, name=f"data_codes_{h}", align_bytes=64)
+            ds = keep.tile([P, NH], U8, name=f"data_scales_{h}", align_bytes=64)
+            data_grouped.append(dg)
+            data_codes.append(dc)
+            data_scales.append(ds)
+
+        def data_interleave(copy, h, n0, n1):
+            source = data_raw[:, :, NH * h + n0 : NH * h + n1]
+            copy(out=data_grouped[h][:, n0:n1, :], in_=source.rearrange("p t n -> p n t"))
+
+        def data_quantize(h):
+            nc.vector.quantize_mx(
+                out=data_codes[h][:].bitcast(FP8X4),
+                scales=data_scales[h][:],
+                in_=data_grouped[h][:].rearrange("p n t -> p (n t)"),
+            )
+
+        permuted = {}
+        grouped = {}
+        code_ops = {}
+        sums = {}
+        masked = {}
+        coded = {}
+        coded_grouped = {}
+        coded_ops = {}
+
+        def product(tile, g0=0, g1=OLD_PASSES):
+            k = slice(K_PASS * g0, K_PASS * g1)
+            nc.vector.tensor_tensor(
+                out=code_rows[tile // 2][:, tile % 2, K1 + K_PASS * g0 : K1 + K_PASS * g1],
+                in0=old_bytes[tile // 2][:, tile % 2, k].bitcast(FP8),
+                in1=scale_all[:, k],
+                op=MULT,
+            )
+
+        def permute(tile):
+            pm = work.tile([P, PASSES, 2, P], F32, name=f"permuted_{tile}", tag="permuted", bufs=3)
+            words = code_rows[tile // 2][:, tile % 2, :].bitcast(F32)
+            nc.scalar.copy(out=pm[:], in_=words.rearrange("p (g w u) -> p g u w", g=PASSES, u=2))
+            permuted[tile] = pm
+
+        def code_transposes(tile):
+            gr = work.tile([P, PASSES, P, PACK], BF16, name=f"grouped_{tile}", tag="grouped", bufs=3, align_bytes=64)
+            grouped[tile] = gr
+            for g0 in (0, 2):
+                bank = psum.tile([P, 2, 2, P], F32, name=f"code_bank_{tile}_{g0}", tag="code_bank", bufs=2)
+                for s in range(2):
+                    g = g0 + s
+                    for u in range(2):
+                        if tile in permuted:
+                            words = permuted[tile][:, g, u, :]
+                        else:
+                            row = code_rows[tile // 2][:, tile % 2, K_PASS * g : K_PASS * (g + 1)]
+                            words = row.bitcast(F32)[:, u : K_PASS // 2 : 2]
+                        nc.tensor.transpose(bank[:, s, u, :], words, ident[:])
+                nc.scalar.copy(out=gr[:, g0 : g0 + 2, :, :].bitcast(F32), in_=bank[:].rearrange("p s u m -> p s m u"))
+
+        def code_quantize(tile, g0=0, g1=PASSES):
+            if g0 == 0:
+                codes = work.tile([P, PASSES, P], U32, name=f"code_codes_{tile}", tag="code_codes", bufs=3, align_bytes=64)
+                scales = work.tile([P, PASSES, P], U8, name=f"code_scales_{tile}", tag="code_scales", bufs=3, align_bytes=64)
+                code_ops[tile] = (codes, scales)
+            codes, scales = code_ops[tile]
+            nc.vector.quantize_mx(
+                out=codes[:, g0:g1, :].rearrange("p g m -> p (g m)").bitcast(FP8X4),
+                scales=scales[:, g0:g1, :].rearrange("p g m -> p (g m)"),
+                in_=grouped[tile][:, g0:g1, :, :].rearrange("p g m t -> p (g m t)"),
+            )
+
+        def stage1(tile, h):
+            acc = psum.tile([P, NH], F32, name=f"stage1_{tile}_{h}", tag="acc", bufs=5)
+            codes, scales = code_ops[tile]
+            order = [1, 0, 2, 3] if h == 0 else [1, 2, 3, 0]
+            for n, g in enumerate(order):
+                if g == 0:
+                    rhs = data_codes[h][:].bitcast(FP8X4)
+                    rhs_scale = data_scales[h][:]
+                else:
+                    rhs = old_code[h][:, g - 1, :].bitcast(FP4X4)
+                    rhs_scale = old_plane[:, g - 1, NH * h : NH * (h + 1)]
+                nc.tensor.matmul_mx(
+                    out=acc[:],
+                    lhsT=codes[:, g, :].bitcast(FP8X4),
+                    lhsT_scale=scales[:, g, :],
+                    rhs=rhs,
+                    rhs_scale=rhs_scale,
+                    start=(n == 0),
+                    stop=(n == PASSES - 1),
+                )
+            sums[tile, h] = acc
+
+        def evacuate(tile, h):
+            copy = work.tile([P, NH], F32, name=f"sum_{tile}_{h}", tag="sum", bufs=1)
+            nc.scalar.copy(out=copy[:], in_=sums[tile, h][:])
+            sums[tile, h] = copy
+
+        def add_mask(tile, h):
+            if h == 0:
+                mt = work.tile([P, F], F32, name=f"masked_{tile}", tag="masked", bufs=2)
+                masked[tile] = mt
+            cols = slice(NH * h, NH * (h + 1))
+            nc.vector.tensor_tensor(
+                out=masked[tile][:, cols], in0=sums[tile, h][:], in1=mask_tiles[tile // 2][:, tile % 2, cols], op=ADD
+            )
+
+        def scale_features(tile):
+            c = work.tile([P, 2, F // PACK, 2], BF16, name=f"coded_{tile}", tag="coded", bufs=2, align_bytes=64)
+            nc.vector.tensor_tensor(
+                out=c[:],
+                in0=masked[tile][:].rearrange("p (w u e) -> p u w e", u=2, e=2),
+                in1=feature_all[:].rearrange("p (w u e) -> p u w e", u=2, e=2),
+                op=MULT,
+            )
+            coded[tile] = c
+
+        def coded_transposes(copy, tile):
+            bank = psum.tile([P, X_PASSES, 2, P], F32, name=f"coded_bank_{tile}", tag="coded_bank", bufs=1)
+            words = coded[tile][:].rearrange("p u w e -> p (u w e)").bitcast(F32)
+            for g in range(X_PASSES):
+                for u in range(2):
+                    first = (X_PASSES * u + g) * P
+                    nc.tensor.transpose(bank[:, g, u, :], words[:, first : first + P], ident[:])
+            cg = work.tile([P, X_PASSES, P, PACK], BF16, name=f"coded_grouped_{tile}", tag="coded_grouped", bufs=2, align_bytes=64)
+            copy(out=cg[:].bitcast(F32), in_=bank[:].rearrange("p g u m -> p g m u"))
+            coded_grouped[tile] = cg
+
+        def coded_quantize(tile):
+            codes = work.tile([P, X_PASSES, P], U32, name=f"coded_codes_{tile}", tag="coded_codes", bufs=2, align_bytes=64)
+            scales = work.tile([P, X_PASSES, P], U8, name=f"coded_scales_{tile}", tag="coded_scales", bufs=2, align_bytes=64)
+            nc.vector.quantize_mx(
+                out=codes[:].rearrange("p g m -> p (g m)").bitcast(FP8X4),
+                scales=scales[:].rearrange("p g m -> p (g m)"),
+                in_=coded_grouped[tile][:].rearrange("p g m t -> p (g m t)"),
+            )
+            coded_ops[tile] = (codes, scales)
+
+        def stage2(tile, on_vector=()):
+            codes, scales = coded_ops[tile]
+            result = work.tile([P, B], F32, name=f"result_{tile}", tag="result", bufs=3)
+            blocks = 1 if tile == TILES - 1 else 2
+            for b in range(X_BLOCKS):
+                cols = slice(NH * b, NH * (b + 1))
+                acc = psum.tile([P, NH], F32, name=f"stage2_{tile}_{b}", tag="acc", bufs=5)
+                for g in range(X_PASSES):
+                    nc.tensor.matmul_mx(
+                        out=acc[:],
+                        lhsT=codes[:, g, :].bitcast(FP8X4),
+                        lhsT_scale=scales[:, g, :],
+                        rhs=x_code[g][:, FP4_BYTES * NH * b : FP4_BYTES * NH * (b + 1)].bitcast(FP4X4),
+                        rhs_scale=x_plane[:, g, cols],
+                        start=(g == 0),
+                        stop=(g == X_PASSES - 1),
+                    )
+                copy = vector_copy if b in on_vector else scalar_copy
+                copy(out=result[:, cols], in_=acc[:])
+                if (b + 1) % blocks == 0:
+                    stored = slice(NH * (b + 1 - blocks), NH * (b + 1))
+                    nc.sync.dma_start(out=out_rows[tile // 2, tile % 2, :, stored], in_=result[:, stored])
+
+        def warm_up(count):
+            bank = psum.tile([P, NH], F32, name="warm_up", tag="acc", bufs=5)
+            rows = code_rows[0][:, 0, 0:NH]
+            for n in range(count):
+                nc.tensor.matmul(bank[:], lhsT=rows[:, 0:P], rhs=rows, start=True, stop=True)
+
+        for g in range(OLD_PASSES):
+            product(0, g, g + 1)
+        code_transposes(0)
+        data_interleave(scalar_copy, 0, 0, NH // 2)
+        data_interleave(vector_copy, 0, NH // 2, NH)
+        spread_features(0)
+        spread_features(1)
+        product(1)
+        warm_up(6)
+        data_interleave(scalar_copy, 1, 0, NH)
+        code_transposes(1)
+        product(3)
+        code_quantize(0, 0, 2)
+        code_quantize(0, 2, 4)
+        data_quantize(0)
+        permute(3)
+        product(2)
+        data_quantize(1)
+        stage1(0, 0)
+        stage1(0, 1)
+        add_mask(0, 0)
+        code_quantize(1)
+        code_transposes(2)
+        stage1(1, 0)
+        stage1(1, 1)
+        add_mask(0, 1)
+        scale_features(0)
+        code_quantize(2)
+        coded_transposes(scalar_copy, 0)
+        code_transposes(3)
+        add_mask(1, 0)
+        add_mask(1, 1)
+        stage1(2, 1)
+        product(4)
+        coded_quantize(0)
+        stage1(2, 0)
+        scale_features(1)
+        code_quantize(3)
+        evacuate(2, 1)
+        add_mask(2, 0)
+        permute(4)
+        add_mask(2, 1)
+        stage2(0, on_vector=(3,))
+        coded_transposes(scalar_copy, 1)
+        scale_features(2)
+        coded_quantize(1)
+
+        for i in range(3, TILES - 1):
+            stage1(i, 0)
+            add_mask(i, 0)
+            code_transposes(i + 1)
+            if i + 2 < TILES:
+                product(i + 2)
+            coded_transposes(scalar_copy, i - 1)
+            stage1(i, 1)
+            code_quantize(i + 1)
+            add_mask(i, 1)
+            if i + 2 < TILES:
+                permute(i + 2)
+            stage2(i - 2)
+            coded_quantize(i - 1)
+            scale_features(i)
+
+        last = TILES - 1
+        stage1(last, 0)
+        stage1(last, 1)
+        coded_transposes(scalar_copy, last - 1)
+        add_mask(last, 0)
+        add_mask(last, 1)
+        scale_features(last)
+        stage2(last - 2)
+        coded_quantize(last - 1)
+        coded_transposes(vector_copy, last)
+        coded_quantize(last)
+        stage2(last - 1, on_vector=(2,))
+        stage2(last, on_vector=(2,))

@@ -326,12 +326,6 @@ def tile_coded_worker_products_s3_kernel(
                     stored = slice(NH * (b + 1 - blocks), NH * (b + 1))
                     nc.sync.dma_start(out=out_rows[tile // 2, tile % 2, :, stored], in_=result[:, stored])
 
-        def warm_up(count):
-            bank = psum.tile([P, NH], F32, name="warm_up", tag="acc", bufs=5)
-            rows = code_rows[0][:, 0, 0:NH]
-            for n in range(count):
-                nc.tensor.matmul(bank[:], lhsT=rows[:, 0:P], rhs=rows, start=True, stop=True)
-
         for g in range(OLD_PASSES):
             product(0, g, g + 1)
         code_transposes(0)
@@ -340,7 +334,6 @@ def tile_coded_worker_products_s3_kernel(
         spread_features(0)
         spread_features(1)
         product(1)
-        warm_up(6)
         data_interleave(scalar_copy, 1, 0, NH)
         code_transposes(1)
         product(3)

@@ -27,9 +27,11 @@ TILES = M // P
 PAIRS = TILES // 2
 HALVES = F // NH
 OLD_PASSES = K2 // K_PASS
-PASSES = (K1 + K2) // K_PASS
+PASSES = OLD_PASSES + 1
+NEW_PASS = OLD_PASSES
 X_PASSES = F // K_PASS
 X_BLOCKS = B // NH
+BANKS = 8
 
 
 def tile_coded_worker_products_s3_kernel(
@@ -44,23 +46,30 @@ def tile_coded_worker_products_s3_kernel(
         psum = ctx.enter_context(tc.psum_pool(name="psum", bufs=1))
         ctx.enter_context(tc.manual_schedule())
 
-        old_plane = keep.tile([P, OLD_PASSES, F], U8, align_bytes=64)
-        x_plane = keep.tile([P, X_PASSES, B], U8, align_bytes=64)
-        primer = keep.tile([P, 2], F32)
+        free_banks = list(range(BANKS))
+        held = {}
+
+        def take_bank(key, shape):
+            b = free_banks.pop(0)
+            held[key] = b
+            bank = psum.tile(shape, F32, name=f"psum_{key}", tag=f"bank_{b}", bufs=1)
+            return bank
+
+        def give_bank(key):
+            free_banks.append(held[key])
+
+        old_plane = keep.tile([P, OLD_PASSES, F], U8, name="old_plane", align_bytes=64)
+        x_plane = keep.tile([P, X_PASSES, B], U8, name="x_plane", align_bytes=64)
+        primer = keep.tile([P, 2], F32, name="primer")
         nc.vector.memset(primer[:], 0.0)
+        ones = keep.tile([P, 1], F32, name="ones")
+        nc.vector.memset(ones[:], 1.0)
         nc.vector.memset(old_plane[:].rearrange("p g n -> p (g n)").bitcast(I32), 0)
         nc.vector.memset(x_plane[:].rearrange("p g n -> p (g n)").bitcast(I32), 0)
 
-        scale_cols = []
-        for g in range(OLD_PASSES):
-            cols = keep.tile([P, PACK], F32, name=f"scale_cols_{g}")
-            nc.scalar.dma_start(out=cols[:], in_=code_old_scale.rearrange("o (g p c) -> g p (o c)", p=P, c=PACK)[g])
-            scale_cols.append(cols)
-        feature_cols_f32 = keep.tile([P, HALVES, PACK], F32)
-        feature_cols = keep.tile([P, HALVES, PACK], BF16)
-        nc.scalar.dma_start(out=feature_cols[:], in_=feature_scale.rearrange("(g p c) -> p g c", p=P, c=PACK))
-        nc.scalar.copy(out=primer[:, 1:2], in_=primer[:, 0:1])
-        ident = keep.tile([P, P], F32)
+        scale_cols = keep.tile([P, OLD_PASSES, PACK], F32, name="scale_cols")
+        feature_cols = keep.tile([P, 2 * PACK], BF16, name="feature_cols")
+        ident = keep.tile([P, P], F32, name="ident")
         make_identity(nc, ident[:])
 
         old_rows = code_old_bytes.rearrange("(j p i) k -> j p i k", p=P, i=2)
@@ -69,98 +78,93 @@ def tile_coded_worker_products_s3_kernel(
         out_rows = out.rearrange("(j p i) b -> j i p b", p=P, i=2)
 
         old_bytes = []
-        code_rows = []
+        new_code = []
         mask_tiles = []
         for j in range(PAIRS):
             ob = keep.tile([P, 2, K2], U8, name=f"old_bytes_{j}")
-            cr = keep.tile([P, 2, K1 + K2], BF16, name=f"code_rows_{j}", align_bytes=64)
+            nw = keep.tile([P, 2 * K1], BF16, name=f"new_code_{j}", align_bytes=64)
             mk = keep.tile([P, 2, F], BF16, name=f"mask_{j}")
             old_bytes.append(ob)
-            code_rows.append(cr)
+            new_code.append(nw)
             mask_tiles.append(mk)
-        data_raw = keep.tile([P, PACK, F], BF16)
-        old_code = []
+        data_raw = []
         for h in range(HALVES):
-            oc = keep.tile([P, OLD_PASSES, FP4_BYTES * NH], U8, name=f"old_code_{h}", align_bytes=64)
+            dr = keep.tile([P, PACK, NH], BF16, name=f"data_raw_{h}")
+            data_raw.append(dr)
+        old_code = []
+        for g in range(OLD_PASSES):
+            oc = keep.tile([P, FP4_BYTES * F], U8, name=f"old_code_{g}", align_bytes=64)
             old_code.append(oc)
         x_code = []
         for g in range(X_PASSES):
             xc = keep.tile([P, FP4_BYTES * B], U8, name=f"x_code_{g}", align_bytes=64)
             x_code.append(xc)
 
-        def load_first_pair(i):
-            nc.sync.dma_start(out=old_bytes[0][:, i, :], in_=old_rows[0, :, i, :])
-            nc.sync.dma_start(out=code_rows[0][:, i, 0:K1], in_=new_rows[0, :, i, :])
+        def prime():
+            nc.scalar.copy(out=primer[:, 1:2], in_=primer[:, 0:1])
 
-        def load_old_pair(j):
-            nc.sync.dma_start(out=old_bytes[j][:], in_=old_rows[j])
+        def load_scale_cols(queue):
+            queue.dma_start(out=scale_cols[:], in_=code_old_scale.rearrange("o (g p c) -> p (o g) c", p=P, c=PACK))
 
-        def load_new_pair(j):
-            nc.sync.dma_start(out=code_rows[j][:, :, 0:K1], in_=new_rows[j])
+        def load_feature_cols(queue):
+            queue.dma_start(out=feature_cols[:], in_=feature_scale.rearrange("(p c) -> p c", p=P))
 
-        def load_mask(j):
-            nc.sync.dma_start(out=mask_tiles[j][:], in_=mask_rows[j])
+        def load_old(j, i0=0, i1=2):
+            nc.sync.dma_start(out=old_bytes[j][:, i0:i1, :], in_=old_rows[j, :, i0:i1, :])
 
-        def load_old_code(h):
-            cols = slice(FP4_BYTES * NH * h, FP4_BYTES * NH * (h + 1))
-            nc.sync.dma_start(out=old_code[h][:], in_=old_words.rearrange("g p n -> p g n")[:, :, cols])
+        def load_new(j, i0=0, i1=2):
+            nc.sync.dma_start(
+                out=new_code[j][:, K1 * i0 : K1 * i1], in_=new_rows[j, :, i0:i1, :].rearrange("p i k -> p (i k)")
+            )
+
+        def load_mask(j, i0=0, i1=2):
+            nc.sync.dma_start(out=mask_tiles[j][:, i0:i1, :], in_=mask_rows[j, :, i0:i1, :])
+
+        def load_data(h):
+            rows = data_new.rearrange("(p t) f -> p t f", t=PACK)
+            nc.sync.dma_start(out=data_raw[h][:], in_=rows[:, :, NH * h : NH * (h + 1)])
+
+        def load_old_code(g):
+            nc.sync.dma_start(out=old_code[g][:], in_=old_words[g])
 
         def load_x_code(g):
             nc.sync.dma_start(out=x_code[g][:], in_=x_words[g])
 
         def load_scales(plane, source):
-            for q in range(4):
+            for r in range(4):
                 nc.sync.dma_start(
-                    out=plane[32 * q : 32 * q + 4, :, :].bitcast(I32),
-                    in_=source.rearrange("g q n -> q g n")[4 * q : 4 * q + 4, :, :].bitcast(I32),
+                    out=plane[r:P:32, :, :].bitcast(I32),
+                    in_=source.rearrange("g q n -> q g n")[r:16:4, :, :].bitcast(I32),
                 )
 
-        load_first_pair(0)
-        nc.sync.dma_start(out=data_raw[:], in_=data_new.rearrange("(p t) f -> p t f", t=PACK))
-        load_first_pair(1)
-        load_old_pair(1)
-        load_scales(old_plane, old_scales)
-        load_new_pair(1)
-        load_old_code(0)
-        load_old_code(1)
-        load_mask(0)
-        load_x_code(0)
-        load_old_pair(2)
-        load_new_pair(2)
-        load_x_code(1)
-        load_scales(x_plane, x_scales)
-        load_mask(1)
-        load_old_pair(3)
-        load_new_pair(3)
-        load_mask(2)
-        load_mask(3)
+        scale_all = keep.tile([P, K2], F32, name="scale_all")
+        feature_all = keep.tile([P, 2, F // PACK, 2], BF16, name="feature_all")
+        spread_banks = {}
 
-        scale_all = keep.tile([P, K2], F32)
-        feature_all = keep.tile([P, F], F32)
-
-        def spread(bank, cols):
+        def spread(key, cols):
+            bank = take_bank(f"spread_{key}", [P, PACK, P])
             for c in range(PACK):
                 nc.tensor.transpose(bank[:, c, :], cols[:, c : c + 1].to_broadcast([P, P]), ident[:])
+            spread_banks[key] = bank
 
-        def collect(dst, bank):
-            nc.scalar.copy(out=dst.rearrange("p (n c) -> p n c", c=PACK), in_=bank[:].rearrange("p c n -> p n c"))
+        def spread_scales(g):
+            spread(g, scale_cols[:, g, :])
 
-        scale_banks = []
-        for g in range(OLD_PASSES):
-            if g < 2:
-                bank = psum.tile([P, PACK, P], F32, name=f"scale_bank_{g}", tag="code_bank", bufs=2)
-            else:
-                bank = psum.tile([P, PACK, P], F32, name=f"scale_bank_{g}", tag="coded_bank", bufs=1)
-            spread(bank, scale_cols[g])
-            scale_banks.append(bank)
-        for g in range(OLD_PASSES):
-            collect(scale_all[:, K_PASS * g : K_PASS * (g + 1)], scale_banks[g])
-        nc.scalar.copy(out=feature_cols_f32[:], in_=feature_cols[:])
+        def collect_scales(g, copy=scalar_copy):
+            dst = scale_all[:, K_PASS * g : K_PASS * (g + 1)]
+            copy(out=dst.rearrange("p (n c) -> p n c", c=PACK), in_=spread_banks[g][:].rearrange("p c n -> p n c"))
+            give_bank(f"spread_{g}")
 
-        def spread_features(h):
-            bank = psum.tile([P, PACK, P], F32, name=f"feature_bank_{h}", tag="code_bank", bufs=2)
-            spread(bank, feature_cols_f32[:, h, :])
-            collect(feature_all[:, NH * h : NH * (h + 1)], bank)
+        def spread_features():
+            spread("f", feature_cols[:].bitcast(F32))
+
+        def collect_features(copy=scalar_copy):
+            dst = feature_all[:].rearrange("p u w e -> p (u w e)").bitcast(F32)
+            copy(
+                out=dst.rearrange("p (u n c) -> p u n c", u=2, c=2),
+                in_=spread_banks["f"][:].rearrange("p (c u) n -> p u n c", u=2),
+            )
+            give_bank("spread_f")
 
         data_grouped = []
         data_codes = []
@@ -173,9 +177,8 @@ def tile_coded_worker_products_s3_kernel(
             data_codes.append(dc)
             data_scales.append(ds)
 
-        def data_interleave(copy, h, n0, n1):
-            source = data_raw[:, :, NH * h + n0 : NH * h + n1]
-            copy(out=data_grouped[h][:, n0:n1, :], in_=source.rearrange("p t n -> p n t"))
+        def data_interleave(copy, h, n0=0, n1=NH):
+            copy(out=data_grouped[h][:, n0:n1, :], in_=data_raw[h][:, :, n0:n1].rearrange("p t n -> p n t"))
 
         def data_quantize(h):
             nc.vector.quantize_mx(
@@ -184,114 +187,179 @@ def tile_coded_worker_products_s3_kernel(
                 in_=data_grouped[h][:].rearrange("p n t -> p (n t)"),
             )
 
+        old_rows_bf = {}
         permuted = {}
         grouped = {}
         code_ops = {}
         sums = {}
         masked = {}
         coded = {}
+        coded_banks = {}
         coded_grouped = {}
         coded_ops = {}
+        results = {}
 
         def product(tile, g0=0, g1=OLD_PASSES):
+            if g0 == 0:
+                ob = work.tile([P, K2], BF16, name=f"old_bf_{tile}", tag="old_bf", bufs=3, align_bytes=64)
+                old_rows_bf[tile] = ob
             k = slice(K_PASS * g0, K_PASS * g1)
             nc.vector.tensor_tensor(
-                out=code_rows[tile // 2][:, tile % 2, K1 + K_PASS * g0 : K1 + K_PASS * g1],
-                in0=old_bytes[tile // 2][:, tile % 2, k].bitcast(FP8),
-                in1=scale_all[:, k],
-                op=MULT,
+                out=old_rows_bf[tile][:, k], in0=old_bytes[tile // 2][:, tile % 2, k].bitcast(FP8), in1=scale_all[:, k], op=MULT
             )
 
-        def permute(tile):
-            pm = work.tile([P, PASSES, 2, P], F32, name=f"permuted_{tile}", tag="permuted", bufs=3)
-            words = code_rows[tile // 2][:, tile % 2, :].bitcast(F32)
-            nc.scalar.copy(out=pm[:], in_=words.rearrange("p (g w u) -> p g u w", g=PASSES, u=2))
-            permuted[tile] = pm
+        def new_words(tile):
+            return new_code[tile // 2][:, K1 * (tile % 2) : K1 * (tile % 2 + 1)].bitcast(F32)
 
-        def code_transposes(tile):
-            gr = work.tile([P, PASSES, P, PACK], BF16, name=f"grouped_{tile}", tag="grouped", bufs=3, align_bytes=64)
-            grouped[tile] = gr
-            for g0 in (0, 2):
-                bank = psum.tile([P, 2, 2, P], F32, name=f"code_bank_{tile}_{g0}", tag="code_bank", bufs=2)
-                for s in range(2):
-                    g = g0 + s
-                    for u in range(2):
-                        if tile in permuted:
-                            words = permuted[tile][:, g, u, :]
-                        else:
-                            row = code_rows[tile // 2][:, tile % 2, K_PASS * g : K_PASS * (g + 1)]
-                            words = row.bitcast(F32)[:, u : K_PASS // 2 : 2]
-                        nc.tensor.transpose(bank[:, s, u, :], words, ident[:])
-                nc.scalar.copy(out=gr[:, g0 : g0 + 2, :, :].bitcast(F32), in_=bank[:].rearrange("p s u m -> p s m u"))
+        def permuted_old(tile):
+            if (tile, "old") not in permuted:
+                pm = work.tile([P, 2, OLD_PASSES * P], F32, name=f"permuted_{tile}", tag="permuted", bufs=3)
+                permuted[tile, "old"] = pm
+            return permuted[tile, "old"]
+
+        def permute(tile, copy=scalar_copy):
+            words = old_rows_bf[tile][:].bitcast(F32)
+            copy(out=permuted_old(tile)[:], in_=words.rearrange("p (w u) -> p u w", u=2))
+
+        def widen(tile, g0, g1):
+            pairs = permuted_old(tile)[:, :, P * g0 : P * g1].bitcast(BF16).rearrange("p u (w e) -> p w u e", e=2)
+            source = old_bytes[tile // 2][:, tile % 2, K_PASS * g0 : K_PASS * g1].bitcast(FP8)
+            nc.vector.tensor_scalar(
+                out=pairs, in0=source.rearrange("p (w u e) -> p w u e", u=2, e=2), scalar1=ones[:], scalar2=None, op0=MULT
+            )
+
+        def permute_new(tile, copy=scalar_copy):
+            pm = work.tile([P, 2, P], F32, name=f"permuted_new_{tile}", tag="permuted_new", bufs=3)
+            copy(out=pm[:], in_=new_words(tile).rearrange("p (w u) -> p u w", u=2))
+            permuted[tile, "new"] = pm
+
+        def words_of(tile, g, u):
+            if g == NEW_PASS:
+                if (tile, "new") in permuted:
+                    return permuted[tile, "new"][:, u, :]
+                return new_words(tile)[:, u : 2 * P : 2]
+            if (tile, "old") in permuted:
+                return permuted[tile, "old"][:, u, P * g : P * (g + 1)]
+            return old_rows_bf[tile][:].bitcast(F32)[:, 2 * P * g + u : 2 * P * (g + 1) : 2]
+
+        code_banks = {}
+        unread = {}
+
+        def slots_read(key, count):
+            unread[key] = unread[key] - count
+            if unread[key] == 0:
+                give_bank(key)
+
+        def transposes(*slots):
+            key = f"cb_{slots[0][0]}_{slots[0][1]}"
+            bank = take_bank(key, [P, 2, 2, P])
+            unread[key] = len(slots)
+            for s, (tile, g) in enumerate(slots):
+                for u in range(2):
+                    nc.tensor.transpose(bank[:, s, u, :], words_of(tile, g, u), ident[:])
+                code_banks[tile, g] = (bank, s, key)
+
+        def grouped_of(tile):
+            if tile not in grouped:
+                gr = work.tile([P, PASSES * P * PACK], BF16, name=f"grouped_{tile}", tag="grouped", bufs=3, align_bytes=64)
+                grouped[tile] = gr
+            return grouped[tile]
+
+        def copy_out(tile, g0, g1, copy=scalar_copy):
+            bank, s, key = code_banks[tile, g0]
+            dst = grouped_of(tile)[:, K_PASS * g0 : K_PASS * g1].bitcast(F32)
+            copy(out=dst.rearrange("p (s m u) -> p s m u", m=P, u=2), in_=bank[:, s : s + g1 - g0].rearrange("p s u m -> p s m u"))
+            slots_read(key, g1 - g0)
+
+        def scale_out(tile, g):
+            bank, s, key = code_banks[tile, g]
+            nc.vector.tensor_tensor(
+                out=grouped_of(tile)[:, K_PASS * g : K_PASS * (g + 1)].rearrange("p (m u e) -> p m u e", u=2, e=2),
+                in0=bank[:, s].bitcast(BF16).rearrange("p u (m e) -> p m u e", e=2),
+                in1=scale_cols[:, g, :].rearrange("p (u e) -> p u e", e=2).unsqueeze(1).to_broadcast([P, P, 2, 2]),
+                op=MULT,
+            )
+            slots_read(key, 1)
+
+        def code_transposes(tile, part):
+            transposes((tile, 2 * part), (tile, 2 * part + 1))
+
+        def code_copy(tile, part, copy=scalar_copy):
+            copy_out(tile, 2 * part, 2 * part + 2, copy)
 
         def code_quantize(tile, g0=0, g1=PASSES):
-            if g0 == 0:
-                codes = work.tile([P, PASSES, P], U32, name=f"code_codes_{tile}", tag="code_codes", bufs=3, align_bytes=64)
-                scales = work.tile([P, PASSES, P], U8, name=f"code_scales_{tile}", tag="code_scales", bufs=3, align_bytes=64)
+            if tile not in code_ops:
+                codes = work.tile([P, PASSES * P], U32, name=f"code_codes_{tile}", tag="code_codes", bufs=4, align_bytes=64)
+                scales = work.tile([P, PASSES * P], U8, name=f"code_scales_{tile}", tag="code_scales", bufs=4, align_bytes=64)
                 code_ops[tile] = (codes, scales)
             codes, scales = code_ops[tile]
             nc.vector.quantize_mx(
-                out=codes[:, g0:g1, :].rearrange("p g m -> p (g m)").bitcast(FP8X4),
-                scales=scales[:, g0:g1, :].rearrange("p g m -> p (g m)"),
-                in_=grouped[tile][:, g0:g1, :, :].rearrange("p g m t -> p (g m t)"),
+                out=codes[:, P * g0 : P * g1].bitcast(FP8X4),
+                scales=scales[:, P * g0 : P * g1],
+                in_=grouped[tile][:, K_PASS * g0 : K_PASS * g1],
             )
 
-        def stage1(tile, h):
-            acc = psum.tile([P, NH], F32, name=f"stage1_{tile}_{h}", tag="acc", bufs=5)
+        def stage1_pass(tile, h, g):
+            if g == 0:
+                acc = take_bank(f"s1_{tile}_{h}", [P, NH])
+                sums[tile, h] = acc
             codes, scales = code_ops[tile]
-            order = [1, 0, 2, 3] if h == 0 else [1, 2, 3, 0]
-            for n, g in enumerate(order):
-                if g == 0:
-                    rhs = data_codes[h][:].bitcast(FP8X4)
-                    rhs_scale = data_scales[h][:]
-                else:
-                    rhs = old_code[h][:, g - 1, :].bitcast(FP4X4)
-                    rhs_scale = old_plane[:, g - 1, NH * h : NH * (h + 1)]
-                nc.tensor.matmul_mx(
-                    out=acc[:],
-                    lhsT=codes[:, g, :].bitcast(FP8X4),
-                    lhsT_scale=scales[:, g, :],
-                    rhs=rhs,
-                    rhs_scale=rhs_scale,
-                    start=(n == 0),
-                    stop=(n == PASSES - 1),
-                )
-            sums[tile, h] = acc
+            if g == NEW_PASS:
+                rhs = data_codes[h][:].bitcast(FP8X4)
+                rhs_scale = data_scales[h][:]
+            else:
+                rhs = old_code[g][:, FP4_BYTES * NH * h : FP4_BYTES * NH * (h + 1)].bitcast(FP4X4)
+                rhs_scale = old_plane[:, g, NH * h : NH * (h + 1)]
+            nc.tensor.matmul_mx(
+                out=sums[tile, h][:],
+                lhsT=codes[:, P * g : P * (g + 1)].bitcast(FP8X4),
+                lhsT_scale=scales[:, P * g : P * (g + 1)],
+                rhs=rhs,
+                rhs_scale=rhs_scale,
+                start=(g == 0),
+                stop=(g == NEW_PASS),
+            )
 
-        def evacuate(tile, h):
-            copy = work.tile([P, NH], F32, name=f"sum_{tile}_{h}", tag="sum", bufs=1)
-            nc.scalar.copy(out=copy[:], in_=sums[tile, h][:])
-            sums[tile, h] = copy
+        def stage1(tile, h, g0=0, g1=PASSES):
+            for g in range(g0, g1):
+                stage1_pass(tile, h, g)
 
         def add_mask(tile, h):
-            if h == 0:
+            if tile not in masked:
                 mt = work.tile([P, F], F32, name=f"masked_{tile}", tag="masked", bufs=2)
                 masked[tile] = mt
             cols = slice(NH * h, NH * (h + 1))
             nc.vector.tensor_tensor(
                 out=masked[tile][:, cols], in0=sums[tile, h][:], in1=mask_tiles[tile // 2][:, tile % 2, cols], op=ADD
             )
+            give_bank(f"s1_{tile}_{h}")
 
-        def scale_features(tile):
-            c = work.tile([P, 2, F // PACK, 2], BF16, name=f"coded_{tile}", tag="coded", bufs=2, align_bytes=64)
-            nc.vector.tensor_tensor(
-                out=c[:],
-                in0=masked[tile][:].rearrange("p (w u e) -> p u w e", u=2, e=2),
-                in1=feature_all[:].rearrange("p (w u e) -> p u w e", u=2, e=2),
+        def scale_features(tile, h0=0, h1=HALVES, engine=nc.vector):
+            if tile not in coded:
+                c = work.tile([P, 2, F // PACK, 2], BF16, name=f"coded_{tile}", tag="coded", bufs=2, align_bytes=64)
+                coded[tile] = c
+            w = slice(P * h0, P * h1)
+            engine.tensor_tensor(
+                out=coded[tile][:, :, w, :],
+                in0=masked[tile][:].rearrange("p (w u e) -> p u w e", u=2, e=2)[:, :, w, :],
+                in1=feature_all[:, :, w, :],
                 op=MULT,
             )
-            coded[tile] = c
 
-        def coded_transposes(copy, tile):
-            bank = psum.tile([P, X_PASSES, 2, P], F32, name=f"coded_bank_{tile}", tag="coded_bank", bufs=1)
+        def coded_transposes(tile):
+            bank = take_bank(f"cc_{tile}", [P, X_PASSES, 2, P])
             words = coded[tile][:].rearrange("p u w e -> p (u w e)").bitcast(F32)
             for g in range(X_PASSES):
                 for u in range(2):
                     first = (X_PASSES * u + g) * P
                     nc.tensor.transpose(bank[:, g, u, :], words[:, first : first + P], ident[:])
+            coded_banks[tile] = bank
+
+        def coded_copy(tile, copy=scalar_copy):
             cg = work.tile([P, X_PASSES, P, PACK], BF16, name=f"coded_grouped_{tile}", tag="coded_grouped", bufs=2, align_bytes=64)
-            copy(out=cg[:].bitcast(F32), in_=bank[:].rearrange("p g u m -> p g m u"))
+            copy(out=cg[:].bitcast(F32), in_=coded_banks[tile][:].rearrange("p g u m -> p g m u"))
             coded_grouped[tile] = cg
+            give_bank(f"cc_{tile}")
 
         def coded_quantize(tile):
             codes = work.tile([P, X_PASSES, P], U32, name=f"coded_codes_{tile}", tag="coded_codes", bufs=2, align_bytes=64)
@@ -303,101 +371,210 @@ def tile_coded_worker_products_s3_kernel(
             )
             coded_ops[tile] = (codes, scales)
 
-        def stage2(tile, on_vector=()):
-            codes, scales = coded_ops[tile]
-            result = work.tile([P, B], F32, name=f"result_{tile}", tag="result", bufs=3)
-            blocks = 1 if tile == TILES - 1 else 2
-            for b in range(X_BLOCKS):
-                cols = slice(NH * b, NH * (b + 1))
-                acc = psum.tile([P, NH], F32, name=f"stage2_{tile}_{b}", tag="acc", bufs=5)
-                for g in range(X_PASSES):
-                    nc.tensor.matmul_mx(
-                        out=acc[:],
-                        lhsT=codes[:, g, :].bitcast(FP8X4),
-                        lhsT_scale=scales[:, g, :],
-                        rhs=x_code[g][:, FP4_BYTES * NH * b : FP4_BYTES * NH * (b + 1)].bitcast(FP4X4),
-                        rhs_scale=x_plane[:, g, cols],
-                        start=(g == 0),
-                        stop=(g == X_PASSES - 1),
-                    )
-                copy = vector_copy if b in on_vector else scalar_copy
-                copy(out=result[:, cols], in_=acc[:])
-                if (b + 1) % blocks == 0:
-                    stored = slice(NH * (b + 1 - blocks), NH * (b + 1))
-                    nc.sync.dma_start(out=out_rows[tile // 2, tile % 2, :, stored], in_=result[:, stored])
+        outs = {}
 
-        for g in range(OLD_PASSES):
-            product(0, g, g + 1)
-        code_transposes(0)
-        data_interleave(scalar_copy, 0, 0, NH // 2)
-        data_interleave(vector_copy, 0, NH // 2, NH)
-        spread_features(0)
-        spread_features(1)
-        product(1)
-        data_interleave(scalar_copy, 1, 0, NH)
-        code_transposes(1)
-        product(3)
-        code_quantize(0, 0, 2)
-        code_quantize(0, 2, 4)
-        data_quantize(0)
-        permute(3)
+        def stage2_block(tile, c0, c1, copy=scalar_copy):
+            stage2_mm(tile, c0, c1)
+            y_copy(tile, c0, c1, copy)
+
+        def y_copy(tile, c0, c1, copy=scalar_copy):
+            if tile not in results:
+                rs = work.tile([P, B], F32, name=f"result_{tile}", tag="result", bufs=3)
+                results[tile] = rs
+            copy(out=results[tile][:, c0:c1], in_=outs[tile, c0][:])
+            give_bank(f"s2_{tile}_{c0}")
+
+        def stage2_mm(tile, c0, c1):
+            codes, scales = coded_ops[tile]
+            acc = take_bank(f"s2_{tile}_{c0}", [P, c1 - c0])
+            for g in range(X_PASSES):
+                nc.tensor.matmul_mx(
+                    out=acc[:],
+                    lhsT=codes[:, g, :].bitcast(FP8X4),
+                    lhsT_scale=scales[:, g, :],
+                    rhs=x_code[g][:, FP4_BYTES * c0 : FP4_BYTES * c1].bitcast(FP4X4),
+                    rhs_scale=x_plane[:, g, c0:c1],
+                    start=(g == 0),
+                    stop=(g == X_PASSES - 1),
+                )
+            outs[tile, c0] = acc
+
+        def store(tile, c0, c1):
+            nc.sync.dma_start(out=out_rows[tile // 2, tile % 2, :, c0:c1], in_=results[tile][:, c0:c1])
+
+        def stage2(tile, on_vector=(), blocks=2):
+            for b in range(X_BLOCKS):
+                stage2_block(tile, NH * b, NH * (b + 1), vector_copy if b in on_vector else scalar_copy)
+                if (b + 1) % blocks == 0:
+                    store(tile, NH * (b + 1 - blocks), NH * (b + 1))
+
+
+        load_scale_cols(nc.scalar)
+        prime()
+        load_old(0, 0, 1)
+        load_old(0, 1, 2)
+        load_scales(old_plane, old_scales)
+        load_new(0)
+        load_data(0)
+        load_old_code(0)
+        load_old(1, 0, 1)
+        load_old_code(1)
+        load_old_code(2)
+        load_data(1)
+        load_feature_cols(nc.sync)
+        load_new(1)
+        load_old(1, 1, 2)
+        load_mask(0)
+        load_scales(x_plane, x_scales)
+        load_old(2)
+        load_mask(1)
+        load_x_code(0)
+        load_x_code(1)
+        load_new(2)
+        load_old(3)
+        load_new(3)
+        load_mask(2)
+        load_mask(3)
+
+        widen(0, 0, 1)
+        widen(0, 1, 3)
+        spread_scales(0)
+        collect_scales(0)
+        spread_scales(1)
+        collect_scales(1)
+        transposes((0, 0))
+        spread_scales(2)
+        collect_scales(2)
+        transposes((0, 1), (0, 2))
+        scale_out(0, 0)
+        product(1, 0, 1)
+        transposes((0, 3))
+        copy_out(0, 3, 4)
+        product(1, 1, 2)
+        code_quantize(0, 0, 1)
+        scale_out(0, 1)
+        scale_out(0, 2)
+        transposes((1, 0), (1, 1))
+        product(1, 2, 3)
+        code_quantize(0, 1, 3)
+        code_quantize(0, 3, 4)
+        data_interleave(scalar_copy, 0)
+        stage1(0, 0, 0, 1)
+        stage1(0, 1, 0, 1)
+        transposes((1, 2), (1, 3))
+        copy_out(1, 0, 2)
+        copy_out(1, 2, 4)
+        stage1(0, 0, 1, 3)
+        stage1(0, 1, 1, 3)
         product(2)
-        data_quantize(1)
-        stage1(0, 0)
-        stage1(0, 1)
-        add_mask(0, 0)
+        data_quantize(0)
         code_quantize(1)
-        code_transposes(2)
+        product(3)
+        data_interleave(scalar_copy, 1)
+        spread_features()
+        code_transposes(2, 0)
+        code_transposes(2, 1)
+        code_copy(2, 0)
+        code_copy(2, 1)
+        collect_features()
+        stage1(0, 0, 3, 4)
         stage1(1, 0)
-        stage1(1, 1)
-        add_mask(0, 1)
-        scale_features(0)
+        stage1(1, 1, 0, 3)
+        data_quantize(1)
+        stage1(0, 1, 3, 4)
+        stage1(1, 1, 3, 4)
+        add_mask(0, 0)
         code_quantize(2)
-        coded_transposes(scalar_copy, 0)
-        code_transposes(3)
+        code_transposes(3, 0)
+        code_copy(3, 0)
+        code_transposes(3, 1)
+        code_copy(3, 1)
+        add_mask(0, 1)
         add_mask(1, 0)
         add_mask(1, 1)
-        stage1(2, 1)
-        product(4)
-        coded_quantize(0)
+        scale_features(0)
         stage1(2, 0)
-        scale_features(1)
+        stage1(2, 1)
         code_quantize(3)
-        evacuate(2, 1)
+        coded_transposes(0)
+        coded_copy(0)
+        scale_features(1)
+        stage1(3, 0)
+        stage1(3, 1)
+        product(4)
         add_mask(2, 0)
-        permute(4)
+        coded_quantize(0)
+        coded_transposes(1)
+        coded_copy(1)
+        code_transposes(4, 0)
+        code_copy(4, 0)
+        code_transposes(4, 1)
+        code_copy(4, 1)
         add_mask(2, 1)
-        stage2(0, on_vector=(3,))
-        coded_transposes(scalar_copy, 1)
-        scale_features(2)
+        product(5)
+        stage2(0)
+        permute(5)
+        permute_new(5)
         coded_quantize(1)
-
-        for i in range(3, TILES - 1):
+        code_quantize(4)
+        scale_features(2)
+        add_mask(3, 0)
+        add_mask(3, 1)
+        stage2(1)
+        scale_features(3)
+        stage1(4, 0)
+        coded_transposes(2)
+        coded_copy(2)
+        code_transposes(5, 0)
+        code_copy(5, 0)
+        code_transposes(5, 1)
+        code_copy(5, 1)
+        coded_transposes(3)
+        coded_copy(3)
+        add_mask(4, 0)
+        coded_quantize(2)
+        product(6)
+        stage1(4, 1)
+        code_quantize(5)
+        add_mask(4, 1)
+        permute(6)
+        permute_new(6)
+        stage2(2)
+        coded_quantize(3)
+        scale_features(4)
+        for i in range(5, TILES - 1):
             stage1(i, 0)
             add_mask(i, 0)
-            code_transposes(i + 1)
+            code_transposes(i + 1, 0)
+            code_copy(i + 1, 0)
+            code_transposes(i + 1, 1)
+            code_copy(i + 1, 1)
             if i + 2 < TILES:
                 product(i + 2)
-            coded_transposes(scalar_copy, i - 1)
+            coded_transposes(i - 1)
+            coded_copy(i - 1)
             stage1(i, 1)
             code_quantize(i + 1)
             add_mask(i, 1)
             if i + 2 < TILES:
                 permute(i + 2)
+                permute_new(i + 2)
             stage2(i - 2)
             coded_quantize(i - 1)
             scale_features(i)
-
         last = TILES - 1
         stage1(last, 0)
-        stage1(last, 1)
-        coded_transposes(scalar_copy, last - 1)
         add_mask(last, 0)
+        coded_transposes(last - 1)
+        coded_copy(last - 1)
+        scale_features(last, 0, 1)
+        stage1(last, 1)
         add_mask(last, 1)
-        scale_features(last)
-        stage2(last - 2)
         coded_quantize(last - 1)
-        coded_transposes(vector_copy, last)
+        scale_features(last, 1, 2)
+        stage2(last - 2, blocks=1)
+        coded_transposes(last)
+        coded_copy(last, vector_copy)
         coded_quantize(last)
-        stage2(last - 1, on_vector=(2,))
-        stage2(last, on_vector=(2,))
+        stage2(last - 1, on_vector=(1, 3), blocks=1)
+        stage2(last, on_vector=(1, 3), blocks=1)

@@ -112,6 +112,10 @@ def tile_coded_worker_products_s3_kernel(
         def load_old(j, i0=0, i1=2):
             nc.sync.dma_start(out=old_bytes[j][:, i0:i1, :], in_=old_rows[j, :, i0:i1, :])
 
+        def load_old_part(j, i, g0, g1):
+            k = slice(K_PASS * g0, K_PASS * g1)
+            nc.sync.dma_start(out=old_bytes[j][:, i, k], in_=old_rows[j, :, i, k])
+
         def load_new(j, i0=0, i1=2):
             nc.sync.dma_start(
                 out=new_code[j][:, K1 * i0 : K1 * i1], in_=new_rows[j, :, i0:i1, :].rearrange("p i k -> p (i k)")
@@ -178,7 +182,10 @@ def tile_coded_worker_products_s3_kernel(
             data_scales.append(ds)
 
         def data_interleave(copy, h, n0=0, n1=NH):
-            copy(out=data_grouped[h][:, n0:n1, :], in_=data_raw[h][:, :, n0:n1].rearrange("p t n -> p n t"))
+            copy(
+                out=data_grouped[h][:, n0:n1, :].rearrange("p (c i) t -> p c t i", i=PACK),
+                in_=data_raw[h][:, :, n0:n1].rearrange("p t (c i) -> p c t i", i=PACK),
+            )
 
         def data_quantize(h):
             nc.vector.quantize_mx(
@@ -207,6 +214,11 @@ def tile_coded_worker_products_s3_kernel(
             nc.vector.tensor_tensor(
                 out=old_rows_bf[tile][:, k], in0=old_bytes[tile // 2][:, tile % 2, k].bitcast(FP8), in1=scale_all[:, k], op=MULT
             )
+
+        def cast(tile):
+            ob = work.tile([P, K2], BF16, name=f"old_bf_{tile}", tag="old_bf", bufs=3, align_bytes=64)
+            old_rows_bf[tile] = ob
+            nc.scalar.copy(out=ob[:], in_=old_bytes[tile // 2][:, tile % 2, :].bitcast(FP8))
 
         def new_words(tile):
             return new_code[tile // 2][:, K1 * (tile % 2) : K1 * (tile % 2 + 1)].bitcast(F32)
@@ -399,8 +411,8 @@ def tile_coded_worker_products_s3_kernel(
                 )
             outs[tile, c0] = acc
 
-        def store(tile, c0, c1):
-            nc.sync.dma_start(out=out_rows[tile // 2, tile % 2, :, c0:c1], in_=results[tile][:, c0:c1])
+        def store(tile, c0, c1, queue=nc.sync):
+            queue.dma_start(out=out_rows[tile // 2, tile % 2, :, c0:c1], in_=results[tile][:, c0:c1])
 
         def stage2(tile, on_vector=(), blocks=2):
             for b in range(X_BLOCKS):
@@ -410,135 +422,132 @@ def tile_coded_worker_products_s3_kernel(
 
 
         load_scale_cols(nc.scalar)
+        load_feature_cols(nc.scalar)
         prime()
         load_old(0, 0, 1)
         load_old(0, 1, 2)
-        load_scales(old_plane, old_scales)
         load_new(0)
         load_data(0)
         load_old_code(0)
-        load_old(1, 0, 1)
+        load_scales(old_plane, old_scales)
         load_old_code(1)
+        load_old(1, 0, 1)
         load_old_code(2)
         load_data(1)
-        load_feature_cols(nc.sync)
-        load_new(1)
         load_old(1, 1, 2)
+        load_new(1)
         load_mask(0)
-        load_scales(x_plane, x_scales)
         load_old(2)
+        load_new(2)
+        load_scales(x_plane, x_scales)
         load_mask(1)
         load_x_code(0)
         load_x_code(1)
-        load_new(2)
         load_old(3)
         load_new(3)
         load_mask(2)
         load_mask(3)
 
-        widen(0, 0, 1)
-        widen(0, 1, 3)
-        spread_scales(0)
-        collect_scales(0)
-        spread_scales(1)
-        collect_scales(1)
-        transposes((0, 0))
-        spread_scales(2)
-        collect_scales(2)
+        widen(0, 0, 3)
+        for g in range(OLD_PASSES):
+            spread_scales(g)
+            collect_scales(g)
+            product(1, g, g + 1)
+        spread_features()
+        collect_features()
+        transposes((0, 0), (0, 3))
         transposes((0, 1), (0, 2))
+        code_transposes(1, 0)
+        code_transposes(1, 1)
         scale_out(0, 0)
-        product(1, 0, 1)
-        transposes((0, 3))
-        copy_out(0, 3, 4)
-        product(1, 1, 2)
-        code_quantize(0, 0, 1)
         scale_out(0, 1)
+        code_quantize(0, 0, 1)
         scale_out(0, 2)
-        transposes((1, 0), (1, 1))
-        product(1, 2, 3)
         code_quantize(0, 1, 3)
-        code_quantize(0, 3, 4)
         data_interleave(scalar_copy, 0)
+        copy_out(0, 3, 4)
+        code_copy(1, 0)
+        code_copy(1, 1)
+        data_interleave(scalar_copy, 1)
         stage1(0, 0, 0, 1)
         stage1(0, 1, 0, 1)
-        transposes((1, 2), (1, 3))
-        copy_out(1, 0, 2)
-        copy_out(1, 2, 4)
         stage1(0, 0, 1, 3)
         stage1(0, 1, 1, 3)
         product(2)
-        data_quantize(0)
         code_quantize(1)
+        data_quantize(0)
+        code_quantize(0, 3, 4)
         product(3)
-        data_interleave(scalar_copy, 1)
-        spread_features()
+        data_quantize(1)
         code_transposes(2, 0)
         code_transposes(2, 1)
         code_copy(2, 0)
         code_copy(2, 1)
-        collect_features()
-        stage1(0, 0, 3, 4)
+        permute_new(4)
         stage1(1, 0)
+        stage1(0, 0, 3, 4)
         stage1(1, 1, 0, 3)
-        data_quantize(1)
         stage1(0, 1, 3, 4)
         stage1(1, 1, 3, 4)
+        code_transposes(3, 0)
+        code_transposes(3, 1)
+        code_copy(3, 0)
+        code_copy(3, 1)
+        cast(4)
+        permute(4)
         add_mask(0, 0)
         code_quantize(2)
-        code_transposes(3, 0)
-        code_copy(3, 0)
-        code_transposes(3, 1)
-        code_copy(3, 1)
         add_mask(0, 1)
         add_mask(1, 0)
-        add_mask(1, 1)
         scale_features(0)
+        code_quantize(3)
+        add_mask(1, 1)
         stage1(2, 0)
         stage1(2, 1)
-        code_quantize(3)
+        stage1(3, 0)
+        add_mask(2, 0)
+        scale_features(1)
         coded_transposes(0)
         coded_copy(0)
-        scale_features(1)
-        stage1(3, 0)
-        stage1(3, 1)
-        product(4)
-        add_mask(2, 0)
-        coded_quantize(0)
+        code_transposes(4, 0)
+        code_transposes(4, 1)
         coded_transposes(1)
         coded_copy(1)
-        code_transposes(4, 0)
-        code_copy(4, 0)
-        code_transposes(4, 1)
-        code_copy(4, 1)
-        add_mask(2, 1)
-        product(5)
-        stage2(0)
-        permute(5)
+        copy_out(4, 3, 4)
         permute_new(5)
-        coded_quantize(1)
-        code_quantize(4)
+        stage1(3, 1)
+        add_mask(2, 1)
+        scale_out(4, 0)
+        coded_quantize(0)
         scale_features(2)
+        coded_quantize(1)
+        scale_out(4, 1)
+        scale_out(4, 2)
+        stage2(0)
+        coded_transposes(2)
+        coded_copy(2)
+        product(5)
+        permute(5)
+        code_quantize(4)
         add_mask(3, 0)
         add_mask(3, 1)
         stage2(1)
+        coded_quantize(2)
         scale_features(3)
         stage1(4, 0)
-        coded_transposes(2)
-        coded_copy(2)
+        stage1(4, 1)
+        add_mask(4, 0)
+        product(6)
         code_transposes(5, 0)
         code_copy(5, 0)
         code_transposes(5, 1)
         code_copy(5, 1)
         coded_transposes(3)
         coded_copy(3)
-        add_mask(4, 0)
-        coded_quantize(2)
-        product(6)
-        stage1(4, 1)
-        code_quantize(5)
-        add_mask(4, 1)
         permute(6)
         permute_new(6)
+        code_quantize(5)
+        add_mask(4, 1)
         stage2(2)
         coded_quantize(3)
         scale_features(4)

@@ -576,11 +576,10 @@ def tile_coded_worker_products_s3_kernel(
         add_mask(last, 0)
         coded_transposes(last - 1)
         coded_copy(last - 1)
-        scale_features(last, 0, 1)
         stage1(last, 1)
         add_mask(last, 1)
         coded_quantize(last - 1)
-        scale_features(last, 1, 2)
+        scale_features(last, 0, 2, nc.gpsimd)
         stage2(last - 2, blocks=1)
         coded_transposes(last)
         coded_copy(last, vector_copy)

@@ -273,7 +273,7 @@ def tile_coded_worker_products_s3_kernel(
 
         def grouped_of(tile):
             if tile not in grouped:
-                gr = work.tile([P, PASSES * P * PACK], BF16, name=f"grouped_{tile}", tag="grouped", bufs=3, align_bytes=64)
+                gr = work.tile([P, PASSES * P * PACK], BF16, name=f"grouped_{tile}", tag="grouped", bufs=4, align_bytes=64)
                 grouped[tile] = gr
             return grouped[tile]
 
@@ -338,7 +338,7 @@ def tile_coded_worker_products_s3_kernel(
 
         def add_mask(tile, h):
             if tile not in masked:
-                mt = work.tile([P, F], F32, name=f"masked_{tile}", tag="masked", bufs=2)
+                mt = work.tile([P, F], F32, name=f"masked_{tile}", tag="masked", bufs=4)
                 masked[tile] = mt
             cols = slice(NH * h, NH * (h + 1))
             nc.vector.tensor_tensor(
@@ -348,7 +348,7 @@ def tile_coded_worker_products_s3_kernel(
 
         def scale_features(tile, h0=0, h1=HALVES, engine=nc.vector):
             if tile not in coded:
-                c = work.tile([P, 2, F // PACK, 2], BF16, name=f"coded_{tile}", tag="coded", bufs=2, align_bytes=64)
+                c = work.tile([P, 2, F // PACK, 2], BF16, name=f"coded_{tile}", tag="coded", bufs=5, align_bytes=64)
                 coded[tile] = c
             w = slice(P * h0, P * h1)
             engine.tensor_tensor(
@@ -368,14 +368,14 @@ def tile_coded_worker_products_s3_kernel(
             coded_banks[tile] = bank
 
         def coded_copy(tile, copy=scalar_copy):
-            cg = work.tile([P, X_PASSES, P, PACK], BF16, name=f"coded_grouped_{tile}", tag="coded_grouped", bufs=2, align_bytes=64)
+            cg = work.tile([P, X_PASSES, P, PACK], BF16, name=f"coded_grouped_{tile}", tag="coded_grouped", bufs=3, align_bytes=64)
             copy(out=cg[:].bitcast(F32), in_=coded_banks[tile][:].rearrange("p g u m -> p g m u"))
             coded_grouped[tile] = cg
             give_bank(f"cc_{tile}")
 
         def coded_quantize(tile):
-            codes = work.tile([P, X_PASSES, P], U32, name=f"coded_codes_{tile}", tag="coded_codes", bufs=2, align_bytes=64)
-            scales = work.tile([P, X_PASSES, P], U8, name=f"coded_scales_{tile}", tag="coded_scales", bufs=2, align_bytes=64)
+            codes = work.tile([P, X_PASSES, P], U32, name=f"coded_codes_{tile}", tag="coded_codes", bufs=3, align_bytes=64)
+            scales = work.tile([P, X_PASSES, P], U8, name=f"coded_scales_{tile}", tag="coded_scales", bufs=3, align_bytes=64)
             nc.vector.quantize_mx(
                 out=codes[:].rearrange("p g m -> p (g m)").bitcast(FP8X4),
                 scales=scales[:].rearrange("p g m -> p (g m)"),
@@ -421,26 +421,26 @@ def tile_coded_worker_products_s3_kernel(
                     store(tile, NH * (b + 1 - blocks), NH * (b + 1))
 
 
+        load_old(0, 0, 1)
         load_scale_cols(nc.scalar)
         load_feature_cols(nc.scalar)
         prime()
-        load_old(0, 0, 1)
         load_old(0, 1, 2)
-        load_new(0)
-        load_data(0)
+        load_old(1, 0, 1)
         load_old_code(0)
         load_scales(old_plane, old_scales)
+        load_data(0)
         load_old_code(1)
-        load_old(1, 0, 1)
         load_old_code(2)
-        load_data(1)
+        load_new(0)
         load_old(1, 1, 2)
+        load_data(1)
         load_new(1)
         load_mask(0)
         load_old(2)
         load_new(2)
-        load_scales(x_plane, x_scales)
         load_mask(1)
+        load_scales(x_plane, x_scales)
         load_x_code(0)
         load_x_code(1)
         load_old(3)
@@ -448,141 +448,161 @@ def tile_coded_worker_products_s3_kernel(
         load_mask(2)
         load_mask(3)
 
-        widen(0, 0, 3)
-        for g in range(OLD_PASSES):
-            spread_scales(g)
-            collect_scales(g)
-            product(1, g, g + 1)
+        def scale_tile(tile):
+            for g in range(OLD_PASSES):
+                scale_out(tile, g)
+
+        def finish(tile, h, engine=nc.gpsimd):
+            add_mask(tile, h)
+            scale_features(tile, h, h + 1, engine)
+
+        widen(0, 0, 1)
+        widen(0, 1, 3)
+        widen(1, 0, 3)
+        cast(2)
+        transposes((0, 0))
+        transposes((0, 1), (0, 2))
         spread_features()
         collect_features()
-        transposes((0, 0), (0, 3))
-        transposes((0, 1), (0, 2))
-        code_transposes(1, 0)
-        code_transposes(1, 1)
+        transposes((1, 0), (1, 1))
+        transposes((1, 2), (2, 0))
         scale_out(0, 0)
         scale_out(0, 1)
         code_quantize(0, 0, 1)
         scale_out(0, 2)
+        scale_out(1, 0)
         code_quantize(0, 1, 3)
-        data_interleave(scalar_copy, 0)
-        copy_out(0, 3, 4)
-        code_copy(1, 0)
-        code_copy(1, 1)
-        data_interleave(scalar_copy, 1)
         stage1(0, 0, 0, 1)
         stage1(0, 1, 0, 1)
+        transposes((2, 1), (2, 2))
         stage1(0, 0, 1, 3)
         stage1(0, 1, 1, 3)
-        product(2)
-        code_quantize(1)
+        data_interleave(scalar_copy, 0)
+        scale_out(1, 1)
+        scale_out(1, 2)
+        scale_out(2, 0)
+        code_quantize(1, 0, 3)
+        transposes((0, 3), (1, 3))
+        cast(3)
+        copy_out(0, 3, 4)
+        copy_out(1, 3, 4)
+        data_interleave(scalar_copy, 1)
+        scale_out(2, 1)
+        scale_out(2, 2)
+        stage1(1, 0, 0, 3)
+        stage1(1, 1, 0, 3)
         data_quantize(0)
         code_quantize(0, 3, 4)
-        product(3)
-        data_quantize(1)
-        code_transposes(2, 0)
-        code_transposes(2, 1)
-        code_copy(2, 0)
-        code_copy(2, 1)
-        permute_new(4)
-        stage1(1, 0)
-        stage1(0, 0, 3, 4)
-        stage1(1, 1, 0, 3)
-        stage1(0, 1, 3, 4)
-        stage1(1, 1, 3, 4)
-        code_transposes(3, 0)
-        code_transposes(3, 1)
-        code_copy(3, 0)
-        code_copy(3, 1)
+        code_quantize(1, 3, 4)
+        code_quantize(2, 0, 3)
+        transposes((3, 0), (3, 1))
+        transposes((3, 2))
+        transposes((2, 3), (3, 3))
+        copy_out(2, 3, 4)
+        copy_out(3, 3, 4)
         cast(4)
         permute(4)
+        permute_new(4)
+        cast(5)
+        stage1(0, 0, 3, 4)
+        stage1(1, 0, 3, 4)
+        scale_out(3, 0)
+        scale_out(3, 1)
+        stage1(2, 0, 0, 3)
+        data_quantize(1)
+        code_quantize(2, 3, 4)
+        scale_out(3, 2)
+        stage1(2, 1, 0, 3)
+        stage1(0, 1, 3, 4)
+        stage1(1, 1, 3, 4)
         add_mask(0, 0)
-        code_quantize(2)
-        add_mask(0, 1)
-        add_mask(1, 0)
-        scale_features(0)
         code_quantize(3)
+        scale_features(0, 0, 1, nc.gpsimd)
+        stage1(2, 0, 3, 4)
+        stage1(2, 1, 3, 4)
+        finish(0, 1)
+        add_mask(1, 0)
         add_mask(1, 1)
-        stage1(2, 0)
-        stage1(2, 1)
+        scale_features(1, 0, 1, nc.gpsimd)
+        scale_features(1, 1, 2, nc.gpsimd)
         stage1(3, 0)
-        add_mask(2, 0)
-        scale_features(1)
-        coded_transposes(0)
-        coded_copy(0)
         code_transposes(4, 0)
         code_transposes(4, 1)
+        copy_out(4, 3, 4)
+        permute(5)
+        permute_new(5)
+        scale_tile(4)
+        stage1(3, 1)
+        code_quantize(4)
+        coded_transposes(0)
+        coded_copy(0)
+        finish(2, 0)
+        finish(2, 1)
+        code_transposes(5, 0)
+        code_transposes(5, 1)
+        copy_out(5, 3, 4)
+        permute_new(6)
+        cast(6)
+        permute(6)
+        stage1(4, 0)
+        coded_quantize(0)
+        scale_tile(5)
+        stage1(4, 1)
+        finish(3, 0)
+        code_quantize(5)
+        stage2(0)
+        finish(3, 1)
+        finish(4, 0)
         coded_transposes(1)
         coded_copy(1)
-        copy_out(4, 3, 4)
-        permute_new(5)
-        stage1(3, 1)
-        add_mask(2, 1)
-        scale_out(4, 0)
-        coded_quantize(0)
-        scale_features(2)
+        code_transposes(6, 0)
+        code_transposes(6, 1)
+        copy_out(6, 3, 4)
+        permute_new(7)
+        cast(7)
+        permute(7)
+        finish(4, 1)
         coded_quantize(1)
-        scale_out(4, 1)
-        scale_out(4, 2)
-        stage2(0)
+        scale_tile(6)
+        stage1(5, 0)
+        stage1(5, 1)
+        finish(5, 0)
+        code_quantize(6)
+        finish(5, 1)
+        stage2(1)
         coded_transposes(2)
         coded_copy(2)
-        product(5)
-        permute(5)
-        code_quantize(4)
-        add_mask(3, 0)
-        add_mask(3, 1)
-        stage2(1)
+        code_transposes(7, 0)
+        code_transposes(7, 1)
+        copy_out(7, 3, 4)
+        scale_out(7, 0)
         coded_quantize(2)
-        scale_features(3)
-        stage1(4, 0)
-        stage1(4, 1)
-        add_mask(4, 0)
-        product(6)
-        code_transposes(5, 0)
-        code_copy(5, 0)
-        code_transposes(5, 1)
-        code_copy(5, 1)
-        coded_transposes(3)
-        coded_copy(3)
-        permute(6)
-        permute_new(6)
-        code_quantize(5)
-        add_mask(4, 1)
+        scale_out(7, 1)
+        scale_out(7, 2)
+        stage1(6, 0)
+        stage1(6, 1)
+        finish(6, 0)
+        code_quantize(7)
+        finish(6, 1)
         stage2(2)
+        for tile in (3, 4, 5):
+            coded_transposes(tile)
+            coded_copy(tile)
+        stage1(7, 0)
         coded_quantize(3)
-        scale_features(4)
-        for i in range(5, TILES - 1):
-            stage1(i, 0)
-            add_mask(i, 0)
-            code_transposes(i + 1, 0)
-            code_copy(i + 1, 0)
-            code_transposes(i + 1, 1)
-            code_copy(i + 1, 1)
-            if i + 2 < TILES:
-                product(i + 2)
-            coded_transposes(i - 1)
-            coded_copy(i - 1)
-            stage1(i, 1)
-            code_quantize(i + 1)
-            add_mask(i, 1)
-            if i + 2 < TILES:
-                permute(i + 2)
-                permute_new(i + 2)
-            stage2(i - 2)
-            coded_quantize(i - 1)
-            scale_features(i)
-        last = TILES - 1
-        stage1(last, 0)
-        add_mask(last, 0)
-        coded_transposes(last - 1)
-        coded_copy(last - 1)
-        stage1(last, 1)
-        add_mask(last, 1)
-        coded_quantize(last - 1)
-        scale_features(last, 0, 2, nc.gpsimd)
-        stage2(last - 2, blocks=1)
-        coded_transposes(last)
-        coded_copy(last, vector_copy)
-        coded_quantize(last)
-        stage2(last - 1, on_vector=(1, 3), blocks=1)
-        stage2(last, on_vector=(1, 3), blocks=1)
+        finish(7, 0, nc.vector)
+        stage1(7, 1)
+        coded_quantize(4)
+        finish(7, 1, nc.vector)
+        coded_quantize(5)
+        stage2(3)
+        stage2(4)
+        coded_transposes(6)
+        coded_copy(6, vector_copy)
+        coded_transposes(7)
+        coded_copy(7, vector_copy)
+        coded_quantize(6)
+        coded_quantize(7)
+        stage2(5, blocks=1)
+        stage2(6, on_vector=(1, 3), blocks=1)
+        stage2(7, on_vector=(1, 3), blocks=1)

@@ -425,25 +425,25 @@ def tile_coded_worker_products_s3_kernel(
         load_scale_cols(nc.scalar)
         load_feature_cols(nc.scalar)
         prime()
-        load_old(0, 1, 2)
         load_old(1, 0, 1)
+        load_old(0, 1, 2)
+        load_old(1, 1, 2)
         load_old_code(0)
         load_scales(old_plane, old_scales)
         load_data(0)
         load_old_code(1)
         load_old_code(2)
         load_new(0)
-        load_old(1, 1, 2)
         load_data(1)
         load_new(1)
-        load_mask(0)
         load_old(2)
+        load_mask(0)
         load_new(2)
+        load_old(3)
         load_mask(1)
         load_scales(x_plane, x_scales)
         load_x_code(0)
         load_x_code(1)
-        load_old(3)
         load_new(3)
         load_mask(2)
         load_mask(3)
@@ -458,23 +458,24 @@ def tile_coded_worker_products_s3_kernel(
 
         widen(0, 0, 1)
         widen(0, 1, 3)
-        widen(1, 0, 3)
         cast(2)
         transposes((0, 0))
-        transposes((0, 1), (0, 2))
         spread_features()
         collect_features()
-        transposes((1, 0), (1, 1))
-        transposes((1, 2), (2, 0))
+        cast(3)
+        transposes((0, 1), (0, 2))
         scale_out(0, 0)
-        scale_out(0, 1)
+        widen(1, 0, 3)
         code_quantize(0, 0, 1)
+        transposes((1, 0), (1, 1))
+        stage1(0, 0, 0, 1)
+        stage1(0, 1, 0, 1)
+        transposes((1, 2), (2, 0))
+        transposes((2, 1), (2, 2))
+        scale_out(0, 1)
         scale_out(0, 2)
         scale_out(1, 0)
         code_quantize(0, 1, 3)
-        stage1(0, 0, 0, 1)
-        stage1(0, 1, 0, 1)
-        transposes((2, 1), (2, 2))
         stage1(0, 0, 1, 3)
         stage1(0, 1, 1, 3)
         data_interleave(scalar_copy, 0)
@@ -483,7 +484,7 @@ def tile_coded_worker_products_s3_kernel(
         scale_out(2, 0)
         code_quantize(1, 0, 3)
         transposes((0, 3), (1, 3))
-        cast(3)
+        transposes((3, 0), (3, 1))
         copy_out(0, 3, 4)
         copy_out(1, 3, 4)
         data_interleave(scalar_copy, 1)
@@ -495,54 +496,50 @@ def tile_coded_worker_products_s3_kernel(
         code_quantize(0, 3, 4)
         code_quantize(1, 3, 4)
         code_quantize(2, 0, 3)
-        transposes((3, 0), (3, 1))
         transposes((3, 2))
         transposes((2, 3), (3, 3))
         copy_out(2, 3, 4)
-        copy_out(3, 3, 4)
         cast(4)
-        permute(4)
-        permute_new(4)
-        cast(5)
         stage1(0, 0, 3, 4)
         stage1(1, 0, 3, 4)
         scale_out(3, 0)
         scale_out(3, 1)
         stage1(2, 0, 0, 3)
         data_quantize(1)
+        finish(0, 0)
+        copy_out(3, 3, 4)
+        permute(4)
+        cast(5)
         code_quantize(2, 3, 4)
         scale_out(3, 2)
-        stage1(2, 1, 0, 3)
         stage1(0, 1, 3, 4)
         stage1(1, 1, 3, 4)
-        add_mask(0, 0)
+        stage1(2, 1, 0, 3)
+        add_mask(1, 0)
         code_quantize(3)
-        scale_features(0, 0, 1, nc.gpsimd)
         stage1(2, 0, 3, 4)
         stage1(2, 1, 3, 4)
         finish(0, 1)
-        add_mask(1, 0)
-        add_mask(1, 1)
-        scale_features(1, 0, 1, nc.gpsimd)
-        scale_features(1, 1, 2, nc.gpsimd)
-        stage1(3, 0)
         code_transposes(4, 0)
         code_transposes(4, 1)
         copy_out(4, 3, 4)
         permute(5)
         permute_new(5)
+        stage1(3, 0)
         scale_tile(4)
         stage1(3, 1)
+        finish(1, 1)
         code_quantize(4)
+        scale_features(1, 0, 1, nc.gpsimd)
         coded_transposes(0)
         coded_copy(0)
+        cast(6)
         finish(2, 0)
         finish(2, 1)
         code_transposes(5, 0)
         code_transposes(5, 1)
         copy_out(5, 3, 4)
         permute_new(6)
-        cast(6)
         permute(6)
         stage1(4, 0)
         coded_quantize(0)

@@ -61,6 +61,8 @@ def tile_coded_worker_products_s3_kernel(
         old_plane = keep.tile([P, OLD_PASSES, F], U8, name="old_plane", align_bytes=64)
         x_plane = keep.tile([P, X_PASSES, B], U8, name="x_plane", align_bytes=64)
         primer = keep.tile([P, 2], F32, name="primer")
+        warm = keep.tile([P, NH], BF16, name="warm")
+        nc.vector.memset(warm[:].bitcast(I32), 0)
         nc.vector.memset(primer[:], 0.0)
         ones = keep.tile([P, 1], F32, name="ones")
         nc.vector.memset(ones[:], 1.0)
@@ -411,6 +413,12 @@ def tile_coded_worker_products_s3_kernel(
                 )
             outs[tile, c0] = acc
 
+        def warm_up(count):
+            bank = take_bank("warm", [P, NH])
+            for n in range(count):
+                nc.tensor.matmul(bank[:], lhsT=warm[:, 0:P], rhs=warm[:], start=True, stop=True)
+            give_bank("warm")
+
         def store(tile, c0, c1, queue=nc.sync):
             queue.dma_start(out=out_rows[tile // 2, tile % 2, :, c0:c1], in_=results[tile][:, c0:c1])
 
@@ -459,11 +467,13 @@ def tile_coded_worker_products_s3_kernel(
         widen(0, 0, 1)
         widen(0, 1, 3)
         cast(2)
+        warm_up(4)
         transposes((0, 0))
         spread_features()
         collect_features()
         cast(3)
         transposes((0, 1), (0, 2))
+        warm_up(2)
         scale_out(0, 0)
         widen(1, 0, 3)
         code_quantize(0, 0, 1)

@@ -217,10 +217,12 @@ def tile_coded_worker_products_s3_kernel(
                 out=old_rows_bf[tile][:, k], in0=old_bytes[tile // 2][:, tile % 2, k].bitcast(FP8), in1=scale_all[:, k], op=MULT
             )
 
-        def cast(tile):
-            ob = work.tile([P, K2], BF16, name=f"old_bf_{tile}", tag="old_bf", bufs=3, align_bytes=64)
-            old_rows_bf[tile] = ob
-            nc.scalar.copy(out=ob[:], in_=old_bytes[tile // 2][:, tile % 2, :].bitcast(FP8))
+        def cast(tile, g0=0, g1=OLD_PASSES):
+            if tile not in old_rows_bf:
+                ob = work.tile([P, K2], BF16, name=f"old_bf_{tile}", tag="old_bf", bufs=3, align_bytes=64)
+                old_rows_bf[tile] = ob
+            k = slice(K_PASS * g0, K_PASS * g1)
+            nc.scalar.copy(out=old_rows_bf[tile][:, k], in_=old_bytes[tile // 2][:, tile % 2, k].bitcast(FP8))
 
         def new_words(tile):
             return new_code[tile // 2][:, K1 * (tile % 2) : K1 * (tile % 2 + 1)].bitcast(F32)
@@ -557,30 +559,48 @@ def tile_coded_worker_products_s3_kernel(
         stage1(4, 1)
         finish(3, 0)
         code_quantize(5)
-        stage2(0)
+        stage2_mm(0, 0, 512)
+        stage2_mm(0, 512, 1024)
+        stage2_mm(0, 1024, 1536)
+        stage2_mm(0, 1536, 2048)
+        y_copy(0, 0, 512)
+        y_copy(0, 512, 1024)
+        store(0, 0, 1024)
+        y_copy(0, 1024, 1536)
         finish(3, 1)
         finish(4, 0)
         coded_transposes(1)
         coded_copy(1)
+        y_copy(0, 1536, 2048)
+        store(0, 1024, 2048)
         code_transposes(6, 0)
         code_transposes(6, 1)
         copy_out(6, 3, 4)
         permute_new(7)
         cast(7)
-        permute(7)
-        finish(4, 1)
         coded_quantize(1)
         scale_tile(6)
+        finish(4, 1)
+        code_quantize(6)
         stage1(5, 0)
         stage1(5, 1)
-        finish(5, 0)
-        code_quantize(6)
-        finish(5, 1)
-        stage2(1)
+        stage2_mm(1, 0, 512)
+        stage2_mm(1, 512, 1024)
+        stage2_mm(1, 1024, 1536)
+        stage2_mm(1, 1536, 2048)
+        y_copy(1, 0, 512)
+        permute(7)
+        y_copy(1, 512, 1024)
+        store(1, 0, 1024)
         coded_transposes(2)
         coded_copy(2)
         code_transposes(7, 0)
+        y_copy(1, 1024, 1536)
+        y_copy(1, 1536, 2048)
+        store(1, 1024, 2048)
         code_transposes(7, 1)
+        finish(5, 0)
+        finish(5, 1)
         copy_out(7, 3, 4)
         scale_out(7, 0)
         coded_quantize(2)
@@ -588,9 +608,10 @@ def tile_coded_worker_products_s3_kernel(
         scale_out(7, 2)
         stage1(6, 0)
         stage1(6, 1)
-        finish(6, 0)
+        add_mask(6, 0)
+        add_mask(6, 1)
         code_quantize(7)
-        finish(6, 1)
+        scale_features(6)
         stage2(2)
         for tile in (3, 4, 5):
             coded_transposes(tile)

@@ -23,6 +23,10 @@ K_PASS = P * PACK
 NH = 512
 FP4_BYTES = 2
 
+SCALE_ROWS = 16
+QUADRANT = 32
+BANKS = 8
+
 TILES = M // P
 PAIRS = TILES // 2
 HALVES = F // NH
@@ -31,7 +35,6 @@ PASSES = OLD_PASSES + 1
 NEW_PASS = OLD_PASSES
 X_PASSES = F // K_PASS
 X_BLOCKS = B // NH
-BANKS = 8
 
 
 def tile_coded_worker_products_s3_kernel(
@@ -102,29 +105,14 @@ def tile_coded_worker_products_s3_kernel(
             xc = keep.tile([P, FP4_BYTES * B], U8, name=f"x_code_{g}", align_bytes=64)
             x_code.append(xc)
 
-        def prime():
-            nc.scalar.copy(out=primer[:, 1:2], in_=primer[:, 0:1])
-
-        def load_scale_cols(queue):
-            queue.dma_start(out=scale_cols[:], in_=code_old_scale.rearrange("o (g p c) -> p (o g) c", p=P, c=PACK))
-
-        def load_feature_cols(queue):
-            queue.dma_start(out=feature_cols[:], in_=feature_scale.rearrange("(p c) -> p c", p=P))
-
         def load_old(j, i0=0, i1=2):
             nc.sync.dma_start(out=old_bytes[j][:, i0:i1, :], in_=old_rows[j, :, i0:i1, :])
 
-        def load_old_part(j, i, g0, g1):
-            k = slice(K_PASS * g0, K_PASS * g1)
-            nc.sync.dma_start(out=old_bytes[j][:, i, k], in_=old_rows[j, :, i, k])
+        def load_new(j):
+            nc.sync.dma_start(out=new_code[j][:], in_=new_rows[j].rearrange("p i k -> p (i k)"))
 
-        def load_new(j, i0=0, i1=2):
-            nc.sync.dma_start(
-                out=new_code[j][:, K1 * i0 : K1 * i1], in_=new_rows[j, :, i0:i1, :].rearrange("p i k -> p (i k)")
-            )
-
-        def load_mask(j, i0=0, i1=2):
-            nc.sync.dma_start(out=mask_tiles[j][:, i0:i1, :], in_=mask_rows[j, :, i0:i1, :])
+        def load_mask(j):
+            nc.sync.dma_start(out=mask_tiles[j][:], in_=mask_rows[j])
 
         def load_data(h):
             rows = data_new.rearrange("(p t) f -> p t f", t=PACK)
@@ -137,40 +125,30 @@ def tile_coded_worker_products_s3_kernel(
             nc.sync.dma_start(out=x_code[g][:], in_=x_words[g])
 
         def load_scales(plane, source):
-            for r in range(4):
+            for r in range(PACK):
                 nc.sync.dma_start(
-                    out=plane[r:P:32, :, :].bitcast(I32),
-                    in_=source.rearrange("g q n -> q g n")[r:16:4, :, :].bitcast(I32),
+                    out=plane[r:P:QUADRANT, :, :].bitcast(I32),
+                    in_=source.rearrange("g q n -> q g n")[r:SCALE_ROWS:PACK, :, :].bitcast(I32),
                 )
 
-        scale_all = keep.tile([P, K2], F32, name="scale_all")
         feature_all = keep.tile([P, 2, F // PACK, 2], BF16, name="feature_all")
-        spread_banks = {}
-
-        def spread(key, cols):
-            bank = take_bank(f"spread_{key}", [P, PACK, P])
-            for c in range(PACK):
-                nc.tensor.transpose(bank[:, c, :], cols[:, c : c + 1].to_broadcast([P, P]), ident[:])
-            spread_banks[key] = bank
-
-        def spread_scales(g):
-            spread(g, scale_cols[:, g, :])
-
-        def collect_scales(g, copy=scalar_copy):
-            dst = scale_all[:, K_PASS * g : K_PASS * (g + 1)]
-            copy(out=dst.rearrange("p (n c) -> p n c", c=PACK), in_=spread_banks[g][:].rearrange("p c n -> p n c"))
-            give_bank(f"spread_{g}")
 
         def spread_features():
-            spread("f", feature_cols[:].bitcast(F32))
-
-        def collect_features(copy=scalar_copy):
+            bank = take_bank("spread", [P, PACK, P])
+            words = feature_cols[:].bitcast(F32)
+            for c in range(PACK):
+                nc.tensor.transpose(bank[:, c, :], words[:, c : c + 1].to_broadcast([P, P]), ident[:])
             dst = feature_all[:].rearrange("p u w e -> p (u w e)").bitcast(F32)
-            copy(
-                out=dst.rearrange("p (u n c) -> p u n c", u=2, c=2),
-                in_=spread_banks["f"][:].rearrange("p (c u) n -> p u n c", u=2),
+            nc.scalar.copy(
+                out=dst.rearrange("p (u n c) -> p u n c", u=2, c=2), in_=bank[:].rearrange("p (c u) n -> p u n c", u=2)
             )
-            give_bank("spread_f")
+            give_bank("spread")
+
+        def warm_up(count):
+            bank = take_bank("warm", [P, NH])
+            for n in range(count):
+                nc.tensor.matmul(bank[:], lhsT=warm[:, 0:P], rhs=warm[:], start=True, stop=True)
+            give_bank("warm")
 
         data_grouped = []
         data_codes = []
@@ -183,10 +161,10 @@ def tile_coded_worker_products_s3_kernel(
             data_codes.append(dc)
             data_scales.append(ds)
 
-        def data_interleave(copy, h, n0=0, n1=NH):
-            copy(
-                out=data_grouped[h][:, n0:n1, :].rearrange("p (c i) t -> p c t i", i=PACK),
-                in_=data_raw[h][:, :, n0:n1].rearrange("p t (c i) -> p c t i", i=PACK),
+        def data_interleave(h):
+            nc.scalar.copy(
+                out=data_grouped[h][:].rearrange("p (c i) t -> p c t i", i=PACK),
+                in_=data_raw[h][:].rearrange("p t (c i) -> p c t i", i=PACK),
             )
 
         def data_quantize(h):
@@ -207,22 +185,12 @@ def tile_coded_worker_products_s3_kernel(
         coded_grouped = {}
         coded_ops = {}
         results = {}
+        outs = {}
 
-        def product(tile, g0=0, g1=OLD_PASSES):
-            if g0 == 0:
-                ob = work.tile([P, K2], BF16, name=f"old_bf_{tile}", tag="old_bf", bufs=3, align_bytes=64)
-                old_rows_bf[tile] = ob
-            k = slice(K_PASS * g0, K_PASS * g1)
-            nc.vector.tensor_tensor(
-                out=old_rows_bf[tile][:, k], in0=old_bytes[tile // 2][:, tile % 2, k].bitcast(FP8), in1=scale_all[:, k], op=MULT
-            )
-
-        def cast(tile, g0=0, g1=OLD_PASSES):
-            if tile not in old_rows_bf:
-                ob = work.tile([P, K2], BF16, name=f"old_bf_{tile}", tag="old_bf", bufs=3, align_bytes=64)
-                old_rows_bf[tile] = ob
-            k = slice(K_PASS * g0, K_PASS * g1)
-            nc.scalar.copy(out=old_rows_bf[tile][:, k], in_=old_bytes[tile // 2][:, tile % 2, k].bitcast(FP8))
+        def cast(tile):
+            ob = work.tile([P, K2], BF16, name=f"old_bf_{tile}", tag="old_bf", bufs=3, align_bytes=64)
+            old_rows_bf[tile] = ob
+            nc.scalar.copy(out=ob[:], in_=old_bytes[tile // 2][:, tile % 2, :].bitcast(FP8))
 
         def new_words(tile):
             return new_code[tile // 2][:, K1 * (tile % 2) : K1 * (tile % 2 + 1)].bitcast(F32)
@@ -233,9 +201,14 @@ def tile_coded_worker_products_s3_kernel(
                 permuted[tile, "old"] = pm
             return permuted[tile, "old"]
 
-        def permute(tile, copy=scalar_copy):
+        def permute(tile):
             words = old_rows_bf[tile][:].bitcast(F32)
-            copy(out=permuted_old(tile)[:], in_=words.rearrange("p (w u) -> p u w", u=2))
+            nc.scalar.copy(out=permuted_old(tile)[:], in_=words.rearrange("p (w u) -> p u w", u=2))
+
+        def permute_new(tile):
+            pm = work.tile([P, 2, P], F32, name=f"permuted_new_{tile}", tag="permuted_new", bufs=3)
+            nc.scalar.copy(out=pm[:], in_=new_words(tile).rearrange("p (w u) -> p u w", u=2))
+            permuted[tile, "new"] = pm
 
         def widen(tile, g0, g1):
             pairs = permuted_old(tile)[:, :, P * g0 : P * g1].bitcast(BF16).rearrange("p u (w e) -> p w u e", e=2)
@@ -243,11 +216,6 @@ def tile_coded_worker_products_s3_kernel(
             nc.vector.tensor_scalar(
                 out=pairs, in0=source.rearrange("p (w u e) -> p w u e", u=2, e=2), scalar1=ones[:], scalar2=None, op0=MULT
             )
-
-        def permute_new(tile, copy=scalar_copy):
-            pm = work.tile([P, 2, P], F32, name=f"permuted_new_{tile}", tag="permuted_new", bufs=3)
-            copy(out=pm[:], in_=new_words(tile).rearrange("p (w u) -> p u w", u=2))
-            permuted[tile, "new"] = pm
 
         def words_of(tile, g, u):
             if g == NEW_PASS:
@@ -261,8 +229,8 @@ def tile_coded_worker_products_s3_kernel(
         code_banks = {}
         unread = {}
 
-        def slots_read(key, count):
-            unread[key] = unread[key] - count
+        def slot_read(key):
+            unread[key] = unread[key] - 1
             if unread[key] == 0:
                 give_bank(key)
 
@@ -275,33 +243,34 @@ def tile_coded_worker_products_s3_kernel(
                     nc.tensor.transpose(bank[:, s, u, :], words_of(tile, g, u), ident[:])
                 code_banks[tile, g] = (bank, s, key)
 
+        def code_transposes(tile):
+            transposes((tile, 0), (tile, 1))
+            transposes((tile, 2), (tile, NEW_PASS))
+
         def grouped_of(tile):
             if tile not in grouped:
                 gr = work.tile([P, PASSES * P * PACK], BF16, name=f"grouped_{tile}", tag="grouped", bufs=4, align_bytes=64)
                 grouped[tile] = gr
             return grouped[tile]
 
-        def copy_out(tile, g0, g1, copy=scalar_copy):
-            bank, s, key = code_banks[tile, g0]
-            dst = grouped_of(tile)[:, K_PASS * g0 : K_PASS * g1].bitcast(F32)
-            copy(out=dst.rearrange("p (s m u) -> p s m u", m=P, u=2), in_=bank[:, s : s + g1 - g0].rearrange("p s u m -> p s m u"))
-            slots_read(key, g1 - g0)
-
-        def scale_out(tile, g):
-            bank, s, key = code_banks[tile, g]
-            nc.vector.tensor_tensor(
-                out=grouped_of(tile)[:, K_PASS * g : K_PASS * (g + 1)].rearrange("p (m u e) -> p m u e", u=2, e=2),
-                in0=bank[:, s].bitcast(BF16).rearrange("p u (m e) -> p m u e", e=2),
-                in1=scale_cols[:, g, :].rearrange("p (u e) -> p u e", e=2).unsqueeze(1).to_broadcast([P, P, 2, 2]),
-                op=MULT,
+        def copy_new(tile):
+            bank, s, key = code_banks[tile, NEW_PASS]
+            dst = grouped_of(tile)[:, K_PASS * NEW_PASS :].bitcast(F32)
+            nc.scalar.copy(
+                out=dst.rearrange("p (s m u) -> p s m u", m=P, u=2), in_=bank[:, s : s + 1].rearrange("p s u m -> p s m u")
             )
-            slots_read(key, 1)
+            slot_read(key)
 
-        def code_transposes(tile, part):
-            transposes((tile, 2 * part), (tile, 2 * part + 1))
-
-        def code_copy(tile, part, copy=scalar_copy):
-            copy_out(tile, 2 * part, 2 * part + 2, copy)
+        def scale_out(tile, g0=0, g1=OLD_PASSES):
+            for g in range(g0, g1):
+                bank, s, key = code_banks[tile, g]
+                nc.vector.tensor_tensor(
+                    out=grouped_of(tile)[:, K_PASS * g : K_PASS * (g + 1)].rearrange("p (m u e) -> p m u e", u=2, e=2),
+                    in0=bank[:, s].bitcast(BF16).rearrange("p u (m e) -> p m u e", e=2),
+                    in1=scale_cols[:, g, :].rearrange("p (u e) -> p u e", e=2).unsqueeze(1).to_broadcast([P, P, 2, 2]),
+                    op=MULT,
+                )
+                slot_read(key)
 
         def code_quantize(tile, g0=0, g1=PASSES):
             if tile not in code_ops:
@@ -315,30 +284,27 @@ def tile_coded_worker_products_s3_kernel(
                 in_=grouped[tile][:, K_PASS * g0 : K_PASS * g1],
             )
 
-        def stage1_pass(tile, h, g):
-            if g == 0:
-                acc = take_bank(f"s1_{tile}_{h}", [P, NH])
-                sums[tile, h] = acc
-            codes, scales = code_ops[tile]
-            if g == NEW_PASS:
-                rhs = data_codes[h][:].bitcast(FP8X4)
-                rhs_scale = data_scales[h][:]
-            else:
-                rhs = old_code[g][:, FP4_BYTES * NH * h : FP4_BYTES * NH * (h + 1)].bitcast(FP4X4)
-                rhs_scale = old_plane[:, g, NH * h : NH * (h + 1)]
-            nc.tensor.matmul_mx(
-                out=sums[tile, h][:],
-                lhsT=codes[:, P * g : P * (g + 1)].bitcast(FP8X4),
-                lhsT_scale=scales[:, P * g : P * (g + 1)],
-                rhs=rhs,
-                rhs_scale=rhs_scale,
-                start=(g == 0),
-                stop=(g == NEW_PASS),
-            )
-
         def stage1(tile, h, g0=0, g1=PASSES):
+            codes, scales = code_ops[tile]
             for g in range(g0, g1):
-                stage1_pass(tile, h, g)
+                if g == 0:
+                    acc = take_bank(f"s1_{tile}_{h}", [P, NH])
+                    sums[tile, h] = acc
+                if g == NEW_PASS:
+                    rhs = data_codes[h][:].bitcast(FP8X4)
+                    rhs_scale = data_scales[h][:]
+                else:
+                    rhs = old_code[g][:, FP4_BYTES * NH * h : FP4_BYTES * NH * (h + 1)].bitcast(FP4X4)
+                    rhs_scale = old_plane[:, g, NH * h : NH * (h + 1)]
+                nc.tensor.matmul_mx(
+                    out=sums[tile, h][:],
+                    lhsT=codes[:, P * g : P * (g + 1)].bitcast(FP8X4),
+                    lhsT_scale=scales[:, P * g : P * (g + 1)],
+                    rhs=rhs,
+                    rhs_scale=rhs_scale,
+                    start=(g == 0),
+                    stop=(g == NEW_PASS),
+                )
 
         def add_mask(tile, h):
             if tile not in masked:
@@ -350,7 +316,7 @@ def tile_coded_worker_products_s3_kernel(
             )
             give_bank(f"s1_{tile}_{h}")
 
-        def scale_features(tile, h0=0, h1=HALVES, engine=nc.vector):
+        def scale_features(engine, tile, h0, h1):
             if tile not in coded:
                 c = work.tile([P, 2, F // PACK, 2], BF16, name=f"coded_{tile}", tag="coded", bufs=5, align_bytes=64)
                 coded[tile] = c
@@ -361,6 +327,10 @@ def tile_coded_worker_products_s3_kernel(
                 in1=feature_all[:, :, w, :],
                 op=MULT,
             )
+
+        def finish(tile, h, engine=nc.gpsimd):
+            add_mask(tile, h)
+            scale_features(engine, tile, h, h + 1)
 
         def coded_transposes(tile):
             bank = take_bank(f"cc_{tile}", [P, X_PASSES, 2, P])
@@ -387,54 +357,44 @@ def tile_coded_worker_products_s3_kernel(
             )
             coded_ops[tile] = (codes, scales)
 
-        outs = {}
+        def turn_coded(tile, copy=scalar_copy):
+            coded_transposes(tile)
+            coded_copy(tile, copy)
 
-        def stage2_block(tile, c0, c1, copy=scalar_copy):
-            stage2_mm(tile, c0, c1)
-            y_copy(tile, c0, c1, copy)
-
-        def y_copy(tile, c0, c1, copy=scalar_copy):
-            if tile not in results:
-                rs = work.tile([P, B], F32, name=f"result_{tile}", tag="result", bufs=3)
-                results[tile] = rs
-            copy(out=results[tile][:, c0:c1], in_=outs[tile, c0][:])
-            give_bank(f"s2_{tile}_{c0}")
-
-        def stage2_mm(tile, c0, c1):
+        def stage2_block(tile, b):
             codes, scales = coded_ops[tile]
-            acc = take_bank(f"s2_{tile}_{c0}", [P, c1 - c0])
+            acc = take_bank(f"s2_{tile}_{b}", [P, NH])
             for g in range(X_PASSES):
                 nc.tensor.matmul_mx(
                     out=acc[:],
                     lhsT=codes[:, g, :].bitcast(FP8X4),
                     lhsT_scale=scales[:, g, :],
-                    rhs=x_code[g][:, FP4_BYTES * c0 : FP4_BYTES * c1].bitcast(FP4X4),
-                    rhs_scale=x_plane[:, g, c0:c1],
+                    rhs=x_code[g][:, FP4_BYTES * NH * b : FP4_BYTES * NH * (b + 1)].bitcast(FP4X4),
+                    rhs_scale=x_plane[:, g, NH * b : NH * (b + 1)],
                     start=(g == 0),
                     stop=(g == X_PASSES - 1),
                 )
-            outs[tile, c0] = acc
+            outs[tile, b] = acc
 
-        def warm_up(count):
-            bank = take_bank("warm", [P, NH])
-            for n in range(count):
-                nc.tensor.matmul(bank[:], lhsT=warm[:, 0:P], rhs=warm[:], start=True, stop=True)
-            give_bank("warm")
+        def emit_block(tile, b, copy=scalar_copy, blocks=2):
+            if tile not in results:
+                rs = work.tile([P, B], F32, name=f"result_{tile}", tag="result", bufs=3)
+                results[tile] = rs
+            copy(out=results[tile][:, NH * b : NH * (b + 1)], in_=outs[tile, b][:])
+            give_bank(f"s2_{tile}_{b}")
+            if (b + 1) % blocks == 0:
+                cols = slice(NH * (b + 1 - blocks), NH * (b + 1))
+                nc.sync.dma_start(out=out_rows[tile // 2, tile % 2, :, cols], in_=results[tile][:, cols])
 
-        def store(tile, c0, c1, queue=nc.sync):
-            queue.dma_start(out=out_rows[tile // 2, tile % 2, :, c0:c1], in_=results[tile][:, c0:c1])
-
-        def stage2(tile, on_vector=(), blocks=2):
+        def stage2(tile, copies=(scalar_copy,), blocks=2):
             for b in range(X_BLOCKS):
-                stage2_block(tile, NH * b, NH * (b + 1), vector_copy if b in on_vector else scalar_copy)
-                if (b + 1) % blocks == 0:
-                    store(tile, NH * (b + 1 - blocks), NH * (b + 1))
-
+                stage2_block(tile, b)
+                emit_block(tile, b, copies[b % len(copies)], blocks)
 
         load_old(0, 0, 1)
-        load_scale_cols(nc.scalar)
-        load_feature_cols(nc.scalar)
-        prime()
+        nc.scalar.dma_start(out=scale_cols[:], in_=code_old_scale.rearrange("o (g p c) -> p (o g) c", p=P, c=PACK))
+        nc.scalar.dma_start(out=feature_cols[:], in_=feature_scale.rearrange("(p c) -> p c", p=P))
+        nc.scalar.copy(out=primer[:, 1:2], in_=primer[:, 0:1])
         load_old(1, 0, 1)
         load_old(0, 1, 2)
         load_old(1, 1, 2)
@@ -452,185 +412,161 @@ def tile_coded_worker_products_s3_kernel(
         load_old(3)
         load_mask(1)
         load_scales(x_plane, x_scales)
-        load_x_code(0)
-        load_x_code(1)
+        for g in range(X_PASSES):
+            load_x_code(g)
         load_new(3)
         load_mask(2)
         load_mask(3)
 
-        def scale_tile(tile):
-            for g in range(OLD_PASSES):
-                scale_out(tile, g)
-
-        def finish(tile, h, engine=nc.gpsimd):
-            add_mask(tile, h)
-            scale_features(tile, h, h + 1, engine)
-
         widen(0, 0, 1)
-        widen(0, 1, 3)
+        widen(0, 1, OLD_PASSES)
         cast(2)
         warm_up(4)
         transposes((0, 0))
         spread_features()
-        collect_features()
         cast(3)
         transposes((0, 1), (0, 2))
         warm_up(2)
-        scale_out(0, 0)
-        widen(1, 0, 3)
+        scale_out(0, 0, 1)
+        widen(1, 0, OLD_PASSES)
         code_quantize(0, 0, 1)
         transposes((1, 0), (1, 1))
-        stage1(0, 0, 0, 1)
-        stage1(0, 1, 0, 1)
+        for h in range(HALVES):
+            stage1(0, h, 0, 1)
         transposes((1, 2), (2, 0))
         transposes((2, 1), (2, 2))
-        scale_out(0, 1)
-        scale_out(0, 2)
-        scale_out(1, 0)
-        code_quantize(0, 1, 3)
-        stage1(0, 0, 1, 3)
-        stage1(0, 1, 1, 3)
-        data_interleave(scalar_copy, 0)
-        scale_out(1, 1)
-        scale_out(1, 2)
-        scale_out(2, 0)
-        code_quantize(1, 0, 3)
-        transposes((0, 3), (1, 3))
+        scale_out(0, 1, OLD_PASSES)
+        scale_out(1, 0, 1)
+        code_quantize(0, 1, OLD_PASSES)
+        for g in range(1, OLD_PASSES):
+            for h in range(HALVES):
+                stage1(0, h, g, g + 1)
+        data_interleave(0)
+        scale_out(1, 1, OLD_PASSES)
+        scale_out(2, 0, 1)
+        code_quantize(1, 0, OLD_PASSES)
+        transposes((0, NEW_PASS), (1, NEW_PASS))
         transposes((3, 0), (3, 1))
-        copy_out(0, 3, 4)
-        copy_out(1, 3, 4)
-        data_interleave(scalar_copy, 1)
-        scale_out(2, 1)
-        scale_out(2, 2)
-        stage1(1, 0, 0, 3)
-        stage1(1, 1, 0, 3)
+        copy_new(0)
+        copy_new(1)
+        data_interleave(1)
+        scale_out(2, 1, OLD_PASSES)
+        for h in range(HALVES):
+            stage1(1, h, 0, OLD_PASSES)
+
         data_quantize(0)
-        code_quantize(0, 3, 4)
-        code_quantize(1, 3, 4)
-        code_quantize(2, 0, 3)
+        code_quantize(0, NEW_PASS, PASSES)
+        code_quantize(1, NEW_PASS, PASSES)
+        code_quantize(2, 0, OLD_PASSES)
         transposes((3, 2))
-        transposes((2, 3), (3, 3))
-        copy_out(2, 3, 4)
+        transposes((2, NEW_PASS), (3, NEW_PASS))
+        copy_new(2)
         cast(4)
-        stage1(0, 0, 3, 4)
-        stage1(1, 0, 3, 4)
-        scale_out(3, 0)
-        scale_out(3, 1)
-        stage1(2, 0, 0, 3)
+        stage1(0, 0, NEW_PASS)
+        stage1(1, 0, NEW_PASS)
+        scale_out(3, 0, 2)
+        stage1(2, 0, 0, OLD_PASSES)
         data_quantize(1)
         finish(0, 0)
-        copy_out(3, 3, 4)
+        copy_new(3)
         permute(4)
         cast(5)
-        code_quantize(2, 3, 4)
-        scale_out(3, 2)
-        stage1(0, 1, 3, 4)
-        stage1(1, 1, 3, 4)
-        stage1(2, 1, 0, 3)
+        code_quantize(2, NEW_PASS, PASSES)
+        scale_out(3, 2, OLD_PASSES)
+        stage1(0, 1, NEW_PASS)
+        stage1(1, 1, NEW_PASS)
+        stage1(2, 1, 0, OLD_PASSES)
         add_mask(1, 0)
         code_quantize(3)
-        stage1(2, 0, 3, 4)
-        stage1(2, 1, 3, 4)
+        for h in range(HALVES):
+            stage1(2, h, NEW_PASS)
         finish(0, 1)
-        code_transposes(4, 0)
-        code_transposes(4, 1)
-        copy_out(4, 3, 4)
+
+        code_transposes(4)
+        copy_new(4)
         permute(5)
         permute_new(5)
         stage1(3, 0)
-        scale_tile(4)
+        scale_out(4)
         stage1(3, 1)
         finish(1, 1)
         code_quantize(4)
-        scale_features(1, 0, 1, nc.gpsimd)
-        coded_transposes(0)
-        coded_copy(0)
+        scale_features(nc.gpsimd, 1, 0, 1)
+
+        turn_coded(0)
         cast(6)
         finish(2, 0)
         finish(2, 1)
-        code_transposes(5, 0)
-        code_transposes(5, 1)
-        copy_out(5, 3, 4)
+        code_transposes(5)
+        copy_new(5)
         permute_new(6)
         permute(6)
         stage1(4, 0)
         coded_quantize(0)
-        scale_tile(5)
+        scale_out(5)
         stage1(4, 1)
         finish(3, 0)
         code_quantize(5)
-        stage2_mm(0, 0, 512)
-        stage2_mm(0, 512, 1024)
-        stage2_mm(0, 1024, 1536)
-        stage2_mm(0, 1536, 2048)
-        y_copy(0, 0, 512)
-        y_copy(0, 512, 1024)
-        store(0, 0, 1024)
-        y_copy(0, 1024, 1536)
+        for b in range(X_BLOCKS):
+            stage2_block(0, b)
+        for b in range(X_BLOCKS - 1):
+            emit_block(0, b)
         finish(3, 1)
         finish(4, 0)
-        coded_transposes(1)
-        coded_copy(1)
-        y_copy(0, 1536, 2048)
-        store(0, 1024, 2048)
-        code_transposes(6, 0)
-        code_transposes(6, 1)
-        copy_out(6, 3, 4)
+
+        turn_coded(1)
+        emit_block(0, X_BLOCKS - 1)
+        code_transposes(6)
+        copy_new(6)
         permute_new(7)
         cast(7)
         coded_quantize(1)
-        scale_tile(6)
+        scale_out(6)
         finish(4, 1)
         code_quantize(6)
-        stage1(5, 0)
-        stage1(5, 1)
-        stage2_mm(1, 0, 512)
-        stage2_mm(1, 512, 1024)
-        stage2_mm(1, 1024, 1536)
-        stage2_mm(1, 1536, 2048)
-        y_copy(1, 0, 512)
+        for h in range(HALVES):
+            stage1(5, h)
+        for b in range(X_BLOCKS):
+            stage2_block(1, b)
+        emit_block(1, 0)
         permute(7)
-        y_copy(1, 512, 1024)
-        store(1, 0, 1024)
-        coded_transposes(2)
-        coded_copy(2)
-        code_transposes(7, 0)
-        y_copy(1, 1024, 1536)
-        y_copy(1, 1536, 2048)
-        store(1, 1024, 2048)
-        code_transposes(7, 1)
+        emit_block(1, 1)
+
+        turn_coded(2)
+        transposes((7, 0), (7, 1))
+        emit_block(1, 2)
+        emit_block(1, 3)
+        transposes((7, 2), (7, NEW_PASS))
         finish(5, 0)
         finish(5, 1)
-        copy_out(7, 3, 4)
-        scale_out(7, 0)
+        copy_new(7)
+        scale_out(7, 0, 1)
         coded_quantize(2)
-        scale_out(7, 1)
-        scale_out(7, 2)
-        stage1(6, 0)
-        stage1(6, 1)
-        add_mask(6, 0)
-        add_mask(6, 1)
-        code_quantize(7)
-        scale_features(6)
+        scale_out(7, 1, OLD_PASSES)
+        for h in range(HALVES):
+            stage1(6, h)
+
+        turn_coded(3)
+        turn_coded(4)
+        for h in range(HALVES):
+            add_mask(6, h)
         stage2(2)
-        for tile in (3, 4, 5):
-            coded_transposes(tile)
-            coded_copy(tile)
-        stage1(7, 0)
         coded_quantize(3)
-        finish(7, 0, nc.vector)
-        stage1(7, 1)
+        code_quantize(7)
         coded_quantize(4)
-        finish(7, 1, nc.vector)
-        coded_quantize(5)
+        scale_features(nc.vector, 6, 0, HALVES)
         stage2(3)
+        stage1(7, 0)
+        finish(7, 0, nc.vector)
+        turn_coded(5)
+        turn_coded(6)
         stage2(4)
-        coded_transposes(6)
-        coded_copy(6, vector_copy)
-        coded_transposes(7)
-        coded_copy(7, vector_copy)
+        coded_quantize(5)
         coded_quantize(6)
-        coded_quantize(7)
+        stage1(7, 1)
+        finish(7, 1, nc.vector)
         stage2(5, blocks=1)
-        stage2(6, on_vector=(1, 3), blocks=1)
-        stage2(7, on_vector=(1, 3), blocks=1)
+        turn_coded(7, vector_copy)
+        coded_quantize(7)
+        stage2(6, (scalar_copy, vector_copy), blocks=1)
+        stage2(7, (scalar_copy, vector_copy), blocks=1)

@@ -63,10 +63,8 @@ def tile_coded_worker_products_s3_kernel(
 
         old_plane = keep.tile([P, OLD_PASSES, F], U8, name="old_plane", align_bytes=64)
         x_plane = keep.tile([P, X_PASSES, B], U8, name="x_plane", align_bytes=64)
-        primer = keep.tile([P, 2], F32, name="primer")
         warm = keep.tile([P, NH], BF16, name="warm")
         nc.vector.memset(warm[:].bitcast(I32), 0)
-        nc.vector.memset(primer[:], 0.0)
         ones = keep.tile([P, 1], F32, name="ones")
         nc.vector.memset(ones[:], 1.0)
         nc.vector.memset(old_plane[:].rearrange("p g n -> p (g n)").bitcast(I32), 0)
@@ -394,7 +392,6 @@ def tile_coded_worker_products_s3_kernel(
         load_old(0, 0, 1)
         nc.scalar.dma_start(out=scale_cols[:], in_=code_old_scale.rearrange("o (g p c) -> p (o g) c", p=P, c=PACK))
         nc.scalar.dma_start(out=feature_cols[:], in_=feature_scale.rearrange("(p c) -> p c", p=P))
-        nc.scalar.copy(out=primer[:, 1:2], in_=primer[:, 0:1])
         load_old(1, 0, 1)
         load_old(0, 1, 2)
         load_old(1, 1, 2)

@@ -136,6 +136,9 @@ def tile_coded_worker_products_s3_kernel(
             words = feature_cols[:].bitcast(F32)
             for c in range(PACK):
                 nc.tensor.transpose(bank[:, c, :], words[:, c : c + 1].to_broadcast([P, P]), ident[:])
+            return bank
+
+        def copy_features(bank):
             dst = feature_all[:].rearrange("p u w e -> p (u w e)").bitcast(F32)
             nc.scalar.copy(
                 out=dst.rearrange("p (u n c) -> p u n c", u=2, c=2), in_=bank[:].rearrange("p (c u) n -> p u n c", u=2)
@@ -392,8 +395,8 @@ def tile_coded_worker_products_s3_kernel(
         load_old(0, 0, 1)
         nc.scalar.dma_start(out=scale_cols[:], in_=code_old_scale.rearrange("o (g p c) -> p (o g) c", p=P, c=PACK))
         nc.scalar.dma_start(out=feature_cols[:], in_=feature_scale.rearrange("(p c) -> p c", p=P))
-        load_old(1, 0, 1)
         load_old(0, 1, 2)
+        load_old(1, 0, 1)
         load_old(1, 1, 2)
         load_old_code(0)
         load_scales(old_plane, old_scales)
@@ -417,33 +420,34 @@ def tile_coded_worker_products_s3_kernel(
 
         widen(0, 0, 1)
         widen(0, 1, OLD_PASSES)
-        cast(2)
+        cast(1)
         warm_up(4)
         transposes((0, 0))
-        spread_features()
+        spread = spread_features()
+        cast(2)
         cast(3)
         transposes((0, 1), (0, 2))
         warm_up(2)
-        scale_out(0, 0, 1)
-        widen(1, 0, OLD_PASSES)
+        scale_out(0, 0, 2)
         code_quantize(0, 0, 1)
         transposes((1, 0), (1, 1))
+        scale_out(0, 2, OLD_PASSES)
+        transposes((1, 2), (2, 0))
         for h in range(HALVES):
             stage1(0, h, 0, 1)
-        transposes((1, 2), (2, 0))
-        transposes((2, 1), (2, 2))
-        scale_out(0, 1, OLD_PASSES)
         scale_out(1, 0, 1)
         code_quantize(0, 1, OLD_PASSES)
+        transposes((2, 1), (2, 2))
+        copy_features(spread)
+        transposes((3, 0), (3, 1))
+        scale_out(1, 1, OLD_PASSES)
         for g in range(1, OLD_PASSES):
             for h in range(HALVES):
                 stage1(0, h, g, g + 1)
         data_interleave(0)
-        scale_out(1, 1, OLD_PASSES)
         scale_out(2, 0, 1)
         code_quantize(1, 0, OLD_PASSES)
         transposes((0, NEW_PASS), (1, NEW_PASS))
-        transposes((3, 0), (3, 1))
         copy_new(0)
         copy_new(1)
         data_interleave(1)

@@ -61,8 +61,8 @@ def tile_coded_worker_products_s3_kernel(
         def give_bank(key):
             free_banks.append(held[key])
 
-        old_plane = keep.tile([P, OLD_PASSES, F], U8, name="old_plane", align_bytes=64)
-        x_plane = keep.tile([P, X_PASSES, B], U8, name="x_plane", align_bytes=64)
+        old_plane = keep.tile([P, OLD_PASSES, F], U8, name="old_plane", align_bytes=256)
+        x_plane = keep.tile([P, X_PASSES, B], U8, name="x_plane", align_bytes=256)
         warm = keep.tile([P, NH], BF16, name="warm")
         nc.vector.memset(warm[:].bitcast(I32), 0)
         ones = keep.tile([P, 1], F32, name="ones")
@@ -96,11 +96,11 @@ def tile_coded_worker_products_s3_kernel(
             data_raw.append(dr)
         old_code = []
         for g in range(OLD_PASSES):
-            oc = keep.tile([P, FP4_BYTES * F], U8, name=f"old_code_{g}", align_bytes=64)
+            oc = keep.tile([P, FP4_BYTES * F], U8, name=f"old_code_{g}", align_bytes=256)
             old_code.append(oc)
         x_code = []
         for g in range(X_PASSES):
-            xc = keep.tile([P, FP4_BYTES * B], U8, name=f"x_code_{g}", align_bytes=64)
+            xc = keep.tile([P, FP4_BYTES * B], U8, name=f"x_code_{g}", align_bytes=256)
             x_code.append(xc)
 
         def load_old(j, i0=0, i1=2):
@@ -156,8 +156,8 @@ def tile_coded_worker_products_s3_kernel(
         data_scales = []
         for h in range(HALVES):
             dg = keep.tile([P, NH, PACK], BF16, name=f"data_grouped_{h}", align_bytes=64)
-            dc = keep.tile([P, NH], U32, name=f"data_codes_{h}", align_bytes=64)
-            ds = keep.tile([P, NH], U8, name=f"data_scales_{h}", align_bytes=64)
+            dc = keep.tile([P, NH], U32, name=f"data_codes_{h}", align_bytes=256)
+            ds = keep.tile([P, NH], U8, name=f"data_scales_{h}", align_bytes=256)
             data_grouped.append(dg)
             data_codes.append(dc)
             data_scales.append(ds)
@@ -275,8 +275,8 @@ def tile_coded_worker_products_s3_kernel(
 
         def code_quantize(tile, g0=0, g1=PASSES):
             if tile not in code_ops:
-                codes = work.tile([P, PASSES * P], U32, name=f"code_codes_{tile}", tag="code_codes", bufs=4, align_bytes=64)
-                scales = work.tile([P, PASSES * P], U8, name=f"code_scales_{tile}", tag="code_scales", bufs=4, align_bytes=64)
+                codes = work.tile([P, PASSES * P], U32, name=f"code_codes_{tile}", tag="code_codes", bufs=4, align_bytes=256)
+                scales = work.tile([P, PASSES * P], U8, name=f"code_scales_{tile}", tag="code_scales", bufs=4, align_bytes=256)
                 code_ops[tile] = (codes, scales)
             codes, scales = code_ops[tile]
             nc.vector.quantize_mx(
@@ -306,6 +306,11 @@ def tile_coded_worker_products_s3_kernel(
                     start=(g == 0),
                     stop=(g == NEW_PASS),
                 )
+
+        def stage1_paired(tile, passes=PASSES):
+            for g in range(passes):
+                for h in range(HALVES):
+                    stage1(tile, h, g, g + 1)
 
         def add_mask(tile, h):
             if tile not in masked:
@@ -349,8 +354,8 @@ def tile_coded_worker_products_s3_kernel(
             give_bank(f"cc_{tile}")
 
         def coded_quantize(tile):
-            codes = work.tile([P, X_PASSES, P], U32, name=f"coded_codes_{tile}", tag="coded_codes", bufs=3, align_bytes=64)
-            scales = work.tile([P, X_PASSES, P], U8, name=f"coded_scales_{tile}", tag="coded_scales", bufs=3, align_bytes=64)
+            codes = work.tile([P, X_PASSES, P], U32, name=f"coded_codes_{tile}", tag="coded_codes", bufs=3, align_bytes=256)
+            scales = work.tile([P, X_PASSES, P], U8, name=f"coded_scales_{tile}", tag="coded_scales", bufs=3, align_bytes=256)
             nc.vector.quantize_mx(
                 out=codes[:].rearrange("p g m -> p (g m)").bitcast(FP8X4),
                 scales=scales[:].rearrange("p g m -> p (g m)"),
@@ -377,6 +382,23 @@ def tile_coded_worker_products_s3_kernel(
                 )
             outs[tile, b] = acc
 
+        def stage2_pair(tile, b):
+            codes, scales = coded_ops[tile]
+            for c in (b, b + 1):
+                acc = take_bank(f"s2_{tile}_{c}", [P, NH])
+                outs[tile, c] = acc
+            for g in range(X_PASSES):
+                for c in (b, b + 1):
+                    nc.tensor.matmul_mx(
+                        out=outs[tile, c][:],
+                        lhsT=codes[:, g, :].bitcast(FP8X4),
+                        lhsT_scale=scales[:, g, :],
+                        rhs=x_code[g][:, FP4_BYTES * NH * c : FP4_BYTES * NH * (c + 1)].bitcast(FP4X4),
+                        rhs_scale=x_plane[:, g, NH * c : NH * (c + 1)],
+                        start=(g == 0),
+                        stop=(g == X_PASSES - 1),
+                    )
+
         def emit_block(tile, b, copy=scalar_copy, blocks=2):
             if tile not in results:
                 rs = work.tile([P, B], F32, name=f"result_{tile}", tag="result", bufs=3)
@@ -386,6 +408,12 @@ def tile_coded_worker_products_s3_kernel(
             if (b + 1) % blocks == 0:
                 cols = slice(NH * (b + 1 - blocks), NH * (b + 1))
                 nc.sync.dma_start(out=out_rows[tile // 2, tile % 2, :, cols], in_=results[tile][:, cols])
+
+        def stage2_paired(tile):
+            for b in range(0, X_BLOCKS, 2):
+                stage2_pair(tile, b)
+                emit_block(tile, b)
+                emit_block(tile, b + 1)
 
         def stage2(tile, copies=(scalar_copy,), blocks=2):
             for b in range(X_BLOCKS):
@@ -452,8 +480,7 @@ def tile_coded_worker_products_s3_kernel(
         copy_new(1)
         data_interleave(1)
         scale_out(2, 1, OLD_PASSES)
-        for h in range(HALVES):
-            stage1(1, h, 0, OLD_PASSES)
+        stage1_paired(1, OLD_PASSES)
 
         data_quantize(0)
         code_quantize(0, NEW_PASS, PASSES)
@@ -508,8 +535,8 @@ def tile_coded_worker_products_s3_kernel(
         stage1(4, 1)
         finish(3, 0)
         code_quantize(5)
-        for b in range(X_BLOCKS):
-            stage2_block(0, b)
+        for b in range(0, X_BLOCKS, 2):
+            stage2_pair(0, b)
         for b in range(X_BLOCKS - 1):
             emit_block(0, b)
         finish(3, 1)
@@ -521,16 +548,15 @@ def tile_coded_worker_products_s3_kernel(
         copy_new(6)
         permute_new(7)
         cast(7)
+        permute(7)
         coded_quantize(1)
         scale_out(6)
         finish(4, 1)
         code_quantize(6)
-        for h in range(HALVES):
-            stage1(5, h)
-        for b in range(X_BLOCKS):
-            stage2_block(1, b)
+        stage1_paired(5)
+        for b in range(0, X_BLOCKS, 2):
+            stage2_pair(1, b)
         emit_block(1, 0)
-        permute(7)
         emit_block(1, 1)
 
         turn_coded(2)
@@ -551,17 +577,17 @@ def tile_coded_worker_products_s3_kernel(
         turn_coded(4)
         for h in range(HALVES):
             add_mask(6, h)
-        stage2(2)
+        stage2_paired(2)
         coded_quantize(3)
         code_quantize(7)
         coded_quantize(4)
         scale_features(nc.vector, 6, 0, HALVES)
-        stage2(3)
+        stage2_paired(3)
         stage1(7, 0)
         finish(7, 0, nc.vector)
         turn_coded(5)
         turn_coded(6)
-        stage2(4)
+        stage2_paired(4)
         coded_quantize(5)
         coded_quantize(6)
         stage1(7, 1)

@@ -177,6 +177,7 @@ def tile_coded_worker_products_s3_kernel(
 
         old_rows_bf = {}
         permuted = {}
+        in_order = set()
         grouped = {}
         code_ops = {}
         sums = {}
@@ -202,9 +203,11 @@ def tile_coded_worker_products_s3_kernel(
                 permuted[tile, "old"] = pm
             return permuted[tile, "old"]
 
-        def permute(tile):
-            words = old_rows_bf[tile][:].bitcast(F32)
-            nc.scalar.copy(out=permuted_old(tile)[:], in_=words.rearrange("p (w u) -> p u w", u=2))
+        def permute(tile, g0=0, g1=OLD_PASSES):
+            words = old_rows_bf[tile][:, K_PASS * g0 : K_PASS * g1].bitcast(F32)
+            nc.scalar.copy(out=permuted_old(tile)[:, :, P * g0 : P * g1], in_=words.rearrange("p (w u) -> p u w", u=2))
+            for g in range(g0, g1):
+                in_order.add((tile, g))
 
         def permute_new(tile):
             pm = work.tile([P, 2, P], F32, name=f"permuted_new_{tile}", tag="permuted_new", bufs=3)
@@ -217,13 +220,15 @@ def tile_coded_worker_products_s3_kernel(
             nc.vector.tensor_scalar(
                 out=pairs, in0=source.rearrange("p (w u e) -> p w u e", u=2, e=2), scalar1=ones[:], scalar2=None, op0=MULT
             )
+            for g in range(g0, g1):
+                in_order.add((tile, g))
 
         def words_of(tile, g, u):
             if g == NEW_PASS:
                 if (tile, "new") in permuted:
                     return permuted[tile, "new"][:, u, :]
                 return new_words(tile)[:, u : 2 * P : 2]
-            if (tile, "old") in permuted:
+            if (tile, g) in in_order:
                 return permuted[tile, "old"][:, u, P * g : P * (g + 1)]
             return old_rows_bf[tile][:].bitcast(F32)[:, 2 * P * g + u : 2 * P * (g + 1) : 2]
 
@@ -241,7 +246,7 @@ def tile_coded_worker_products_s3_kernel(
             unread[key] = len(slots)
             for s, (tile, g) in enumerate(slots):
                 for u in range(2):
-                    nc.tensor.transpose(bank[:, s, u, :], words_of(tile, g, u), ident[:])
+                    nc.tensor.transpose(bank[:, u, s, :], words_of(tile, g, u), ident[:])
                 code_banks[tile, g] = (bank, s, key)
 
         def code_transposes(tile):
@@ -258,7 +263,7 @@ def tile_coded_worker_products_s3_kernel(
             bank, s, key = code_banks[tile, NEW_PASS]
             dst = grouped_of(tile)[:, K_PASS * NEW_PASS :].bitcast(F32)
             nc.scalar.copy(
-                out=dst.rearrange("p (s m u) -> p s m u", m=P, u=2), in_=bank[:, s : s + 1].rearrange("p s u m -> p s m u")
+                out=dst.rearrange("p (s m u) -> p s m u", m=P, u=2), in_=bank[:, :, s : s + 1].rearrange("p u s m -> p s m u")
             )
             slot_read(key)
 
@@ -267,11 +272,26 @@ def tile_coded_worker_products_s3_kernel(
                 bank, s, key = code_banks[tile, g]
                 nc.vector.tensor_tensor(
                     out=grouped_of(tile)[:, K_PASS * g : K_PASS * (g + 1)].rearrange("p (m u e) -> p m u e", u=2, e=2),
-                    in0=bank[:, s].bitcast(BF16).rearrange("p u (m e) -> p m u e", e=2),
+                    in0=bank[:, :, s].bitcast(BF16).rearrange("p u (m e) -> p m u e", e=2),
                     in1=scale_cols[:, g, :].rearrange("p (u e) -> p u e", e=2).unsqueeze(1).to_broadcast([P, P, 2, 2]),
                     op=MULT,
                 )
                 slot_read(key)
+
+        def scale_out_both(tile, g):
+            bank, s, key = code_banks[tile, g]
+            nc.vector.tensor_tensor(
+                out=grouped_of(tile)[:, K_PASS * g : K_PASS * (g + 2)].rearrange("p (g m u e) -> p g m u e", g=2, u=2, e=2),
+                in0=bank[:].bitcast(BF16).rearrange("p u g (m e) -> p g m u e", e=2),
+                in1=scale_cols[:, g : g + 2, :].rearrange("p g (u e) -> p g u e", e=2).unsqueeze(2).to_broadcast([P, 2, P, 2, 2]),
+                op=MULT,
+            )
+            slot_read(key)
+            slot_read(key)
+
+        def scale_out_all(tile):
+            scale_out_both(tile, 0)
+            scale_out(tile, 2, OLD_PASSES)
 
         def code_quantize(tile, g0=0, g1=PASSES):
             if tile not in code_ops:
@@ -424,19 +444,18 @@ def tile_coded_worker_products_s3_kernel(
         nc.scalar.dma_start(out=scale_cols[:], in_=code_old_scale.rearrange("o (g p c) -> p (o g) c", p=P, c=PACK))
         nc.scalar.dma_start(out=feature_cols[:], in_=feature_scale.rearrange("(p c) -> p c", p=P))
         load_old(0, 1, 2)
-        load_old(1, 0, 1)
-        load_old(1, 1, 2)
+        load_old(1)
         load_old_code(0)
         load_scales(old_plane, old_scales)
         load_data(0)
         load_old_code(1)
         load_old_code(2)
-        load_new(0)
         load_data(1)
+        load_new(0)
         load_new(1)
         load_old(2)
-        load_mask(0)
         load_new(2)
+        load_mask(0)
         load_old(3)
         load_mask(1)
         load_scales(x_plane, x_scales)
@@ -463,60 +482,59 @@ def tile_coded_worker_products_s3_kernel(
         transposes((1, 2), (2, 0))
         for h in range(HALVES):
             stage1(0, h, 0, 1)
-        scale_out(1, 0, 1)
+        scale_out(1, 0, 2)
         code_quantize(0, 1, OLD_PASSES)
+        code_quantize(1, 0, 2)
         transposes((2, 1), (2, 2))
         copy_features(spread)
         transposes((3, 0), (3, 1))
-        scale_out(1, 1, OLD_PASSES)
-        for g in range(1, OLD_PASSES):
-            for h in range(HALVES):
-                stage1(0, h, g, g + 1)
-        data_interleave(0)
+        permute(3, 2, OLD_PASSES)
+        transposes((3, 2))
+        scale_out(1, 2, OLD_PASSES)
         scale_out(2, 0, 1)
-        code_quantize(1, 0, OLD_PASSES)
-        transposes((0, NEW_PASS), (1, NEW_PASS))
-        copy_new(0)
-        copy_new(1)
+        for tile, g in ((0, 1), (1, 0), (1, 1), (0, 2)):
+            for h in range(HALVES):
+                stage1(tile, h, g, g + 1)
+        data_interleave(0)
         data_interleave(1)
-        scale_out(2, 1, OLD_PASSES)
-        stage1_paired(1, OLD_PASSES)
-
+        code_quantize(1, 2, OLD_PASSES)
+        for h in range(HALVES):
+            stage1(1, h, 2, OLD_PASSES)
+        scale_out_both(2, 1)
+        scale_out(3, 2, OLD_PASSES)
+        code_quantize(2, 0, OLD_PASSES)
+        transposes((0, NEW_PASS), (1, NEW_PASS))
+        transposes((2, NEW_PASS), (3, NEW_PASS))
+        scale_out_both(3, 0)
+        stage1(2, 0, 0, OLD_PASSES)
+        stage1(2, 1, 0, OLD_PASSES)
+        for tile in range(4):
+            copy_new(tile)
         data_quantize(0)
         code_quantize(0, NEW_PASS, PASSES)
         code_quantize(1, NEW_PASS, PASSES)
-        code_quantize(2, 0, OLD_PASSES)
-        transposes((3, 2))
-        transposes((2, NEW_PASS), (3, NEW_PASS))
-        copy_new(2)
-        cast(4)
-        stage1(0, 0, NEW_PASS)
-        stage1(1, 0, NEW_PASS)
-        scale_out(3, 0, 2)
-        stage1(2, 0, 0, OLD_PASSES)
         data_quantize(1)
-        finish(0, 0)
-        copy_new(3)
-        permute(4)
-        cast(5)
         code_quantize(2, NEW_PASS, PASSES)
-        scale_out(3, 2, OLD_PASSES)
-        stage1(0, 1, NEW_PASS)
-        stage1(1, 1, NEW_PASS)
-        stage1(2, 1, 0, OLD_PASSES)
-        add_mask(1, 0)
         code_quantize(3)
+        cast(4)
+        permute_new(4)
+        permute(4, 0, 2)
+        permute(4, 2, OLD_PASSES)
+        cast(5)
+        for h in range(HALVES):
+            for tile in range(2):
+                stage1(tile, h, NEW_PASS)
         for h in range(HALVES):
             stage1(2, h, NEW_PASS)
+        finish(0, 0)
+        add_mask(1, 0)
         finish(0, 1)
-
         code_transposes(4)
         copy_new(4)
         permute(5)
         permute_new(5)
-        stage1(3, 0)
-        scale_out(4)
-        stage1(3, 1)
+        stage1_paired(3)
+        scale_out_all(4)
         finish(1, 1)
         code_quantize(4)
         scale_features(nc.gpsimd, 1, 0, 1)
@@ -531,7 +549,7 @@ def tile_coded_worker_products_s3_kernel(
         permute(6)
         stage1(4, 0)
         coded_quantize(0)
-        scale_out(5)
+        scale_out_all(5)
         stage1(4, 1)
         finish(3, 0)
         code_quantize(5)
@@ -550,7 +568,7 @@ def tile_coded_worker_products_s3_kernel(
         cast(7)
         permute(7)
         coded_quantize(1)
-        scale_out(6)
+        scale_out_all(6)
         finish(4, 1)
         code_quantize(6)
         stage1_paired(5)
@@ -567,18 +585,17 @@ def tile_coded_worker_products_s3_kernel(
         finish(5, 0)
         finish(5, 1)
         copy_new(7)
-        scale_out(7, 0, 1)
         coded_quantize(2)
-        scale_out(7, 1, OLD_PASSES)
+        scale_out_all(7)
         for h in range(HALVES):
             stage1(6, h)
 
         turn_coded(3)
         turn_coded(4)
-        for h in range(HALVES):
-            add_mask(6, h)
-        stage2_paired(2)
+        add_mask(6, 0)
         coded_quantize(3)
+        add_mask(6, 1)
+        stage2_paired(2)
         code_quantize(7)
         coded_quantize(4)
         scale_features(nc.vector, 6, 0, HALVES)

@@ -246,7 +246,7 @@ def tile_coded_worker_products_s3_kernel(
             unread[key] = len(slots)
             for s, (tile, g) in enumerate(slots):
                 for u in range(2):
-                    nc.tensor.transpose(bank[:, u, s, :], words_of(tile, g, u), ident[:])
+                    nc.tensor.transpose(bank[:, s, u, :], words_of(tile, g, u), ident[:])
                 code_banks[tile, g] = (bank, s, key)
 
         def code_transposes(tile):
@@ -263,7 +263,7 @@ def tile_coded_worker_products_s3_kernel(
             bank, s, key = code_banks[tile, NEW_PASS]
             dst = grouped_of(tile)[:, K_PASS * NEW_PASS :].bitcast(F32)
             nc.scalar.copy(
-                out=dst.rearrange("p (s m u) -> p s m u", m=P, u=2), in_=bank[:, :, s : s + 1].rearrange("p u s m -> p s m u")
+                out=dst.rearrange("p (s m u) -> p s m u", m=P, u=2), in_=bank[:, s : s + 1].rearrange("p s u m -> p s m u")
             )
             slot_read(key)
 
@@ -272,26 +272,11 @@ def tile_coded_worker_products_s3_kernel(
                 bank, s, key = code_banks[tile, g]
                 nc.vector.tensor_tensor(
                     out=grouped_of(tile)[:, K_PASS * g : K_PASS * (g + 1)].rearrange("p (m u e) -> p m u e", u=2, e=2),
-                    in0=bank[:, :, s].bitcast(BF16).rearrange("p u (m e) -> p m u e", e=2),
+                    in0=bank[:, s].bitcast(BF16).rearrange("p u (m e) -> p m u e", e=2),
                     in1=scale_cols[:, g, :].rearrange("p (u e) -> p u e", e=2).unsqueeze(1).to_broadcast([P, P, 2, 2]),
                     op=MULT,
                 )
                 slot_read(key)
-
-        def scale_out_both(tile, g):
-            bank, s, key = code_banks[tile, g]
-            nc.vector.tensor_tensor(
-                out=grouped_of(tile)[:, K_PASS * g : K_PASS * (g + 2)].rearrange("p (g m u e) -> p g m u e", g=2, u=2, e=2),
-                in0=bank[:].bitcast(BF16).rearrange("p u g (m e) -> p g m u e", e=2),
-                in1=scale_cols[:, g : g + 2, :].rearrange("p g (u e) -> p g u e", e=2).unsqueeze(2).to_broadcast([P, 2, P, 2, 2]),
-                op=MULT,
-            )
-            slot_read(key)
-            slot_read(key)
-
-        def scale_out_all(tile):
-            scale_out_both(tile, 0)
-            scale_out(tile, 2, OLD_PASSES)
 
         def code_quantize(tile, g0=0, g1=PASSES):
             if tile not in code_ops:
@@ -500,12 +485,12 @@ def tile_coded_worker_products_s3_kernel(
         code_quantize(1, 2, OLD_PASSES)
         for h in range(HALVES):
             stage1(1, h, 2, OLD_PASSES)
-        scale_out_both(2, 1)
+        scale_out(2, 1, 3)
         scale_out(3, 2, OLD_PASSES)
         code_quantize(2, 0, OLD_PASSES)
         transposes((0, NEW_PASS), (1, NEW_PASS))
         transposes((2, NEW_PASS), (3, NEW_PASS))
-        scale_out_both(3, 0)
+        scale_out(3, 0, 2)
         stage1(2, 0, 0, OLD_PASSES)
         stage1(2, 1, 0, OLD_PASSES)
         for tile in range(4):
@@ -534,7 +519,7 @@ def tile_coded_worker_products_s3_kernel(
         permute(5)
         permute_new(5)
         stage1_paired(3)
-        scale_out_all(4)
+        scale_out(4)
         finish(1, 1)
         code_quantize(4)
         scale_features(nc.gpsimd, 1, 0, 1)
@@ -549,7 +534,7 @@ def tile_coded_worker_products_s3_kernel(
         permute(6)
         stage1(4, 0)
         coded_quantize(0)
-        scale_out_all(5)
+        scale_out(5)
         stage1(4, 1)
         finish(3, 0)
         code_quantize(5)
@@ -568,7 +553,7 @@ def tile_coded_worker_products_s3_kernel(
         cast(7)
         permute(7)
         coded_quantize(1)
-        scale_out_all(6)
+        scale_out(6)
         finish(4, 1)
         code_quantize(6)
         stage1_paired(5)
@@ -586,7 +571,7 @@ def tile_coded_worker_products_s3_kernel(
         finish(5, 1)
         copy_new(7)
         coded_quantize(2)
-        scale_out_all(7)
+        scale_out(7)
         for h in range(HALVES):
             stage1(6, h)
 

@@ -177,6 +177,8 @@ def tile_coded_worker_products_s3_kernel(
 
         old_rows_bf = {}
         permuted = {}
+        parts = {}
+        raws = {}
         in_order = set()
         grouped = {}
         code_ops = {}
@@ -253,11 +255,40 @@ def tile_coded_worker_products_s3_kernel(
             transposes((tile, 0), (tile, 1))
             transposes((tile, 2), (tile, NEW_PASS))
 
-        def grouped_of(tile):
+        def grouped_of(tile, tag="grouped", bufs=4):
             if tile not in grouped:
-                gr = work.tile([P, PASSES * P * PACK], BF16, name=f"grouped_{tile}", tag="grouped", bufs=4, align_bytes=64)
+                gr = work.tile([P, PASSES * P * PACK], BF16, name=f"grouped_{tile}", tag=tag, bufs=bufs, align_bytes=64)
                 grouped[tile] = gr
             return grouped[tile]
+
+        def passes_of(tile, g0, g1):
+            if (tile, g0) in parts:
+                part, first = parts[tile, g0]
+                return part[:, K_PASS * (g0 - first) : K_PASS * (g1 - first)]
+            return grouped_of(tile)[:, K_PASS * g0 : K_PASS * g1]
+
+        def own_buffer(tile, g0, g1, tag):
+            part = work.tile([P, K_PASS * (g1 - g0)], BF16, name=f"part_{tile}_{g0}", tag=tag, bufs=1, align_bytes=64)
+            for g in range(g0, g1):
+                parts[tile, g] = (part, g0)
+
+        def copy_raw(tile, g):
+            bank, s, key = code_banks[tile, g]
+            raw = work.tile([P, K_PASS], BF16, name=f"raw_{tile}_{g}", tag="raw", bufs=2)
+            raws[tile, g] = raw
+            nc.scalar.copy(
+                out=raw[:].bitcast(F32).rearrange("p (s m u) -> p s m u", m=P, u=2),
+                in_=bank[:, s : s + 1].rearrange("p s u m -> p s m u"),
+            )
+            slot_read(key)
+
+        def scale_raw(tile, g):
+            nc.gpsimd.tensor_tensor(
+                out=passes_of(tile, g, g + 1).rearrange("p (m t) -> p m t", t=PACK),
+                in0=raws[tile, g][:].rearrange("p (m t) -> p m t", t=PACK),
+                in1=scale_cols[:, g, :].unsqueeze(1).to_broadcast([P, P, PACK]),
+                op=MULT,
+            )
 
         def copy_new(tile):
             bank, s, key = code_banks[tile, NEW_PASS]
@@ -271,7 +302,7 @@ def tile_coded_worker_products_s3_kernel(
             for g in range(g0, g1):
                 bank, s, key = code_banks[tile, g]
                 nc.vector.tensor_tensor(
-                    out=grouped_of(tile)[:, K_PASS * g : K_PASS * (g + 1)].rearrange("p (m u e) -> p m u e", u=2, e=2),
+                    out=passes_of(tile, g, g + 1).rearrange("p (m u e) -> p m u e", u=2, e=2),
                     in0=bank[:, s].bitcast(BF16).rearrange("p u (m e) -> p m u e", e=2),
                     in1=scale_cols[:, g, :].rearrange("p (u e) -> p u e", e=2).unsqueeze(1).to_broadcast([P, P, 2, 2]),
                     op=MULT,
@@ -287,7 +318,7 @@ def tile_coded_worker_products_s3_kernel(
             nc.vector.quantize_mx(
                 out=codes[:, P * g0 : P * g1].bitcast(FP8X4),
                 scales=scales[:, P * g0 : P * g1],
-                in_=grouped[tile][:, K_PASS * g0 : K_PASS * g1],
+                in_=passes_of(tile, g0, g1),
             )
 
         def stage1(tile, h, g0=0, g1=PASSES):
@@ -475,22 +506,26 @@ def tile_coded_worker_products_s3_kernel(
         transposes((3, 0), (3, 1))
         permute(3, 2, OLD_PASSES)
         transposes((3, 2))
+        own_buffer(1, 2, OLD_PASSES, "handover")
         scale_out(1, 2, OLD_PASSES)
         scale_out(2, 0, 1)
         for tile, g in ((0, 1), (1, 0), (1, 1), (0, 2)):
             for h in range(HALVES):
                 stage1(tile, h, g, g + 1)
         data_interleave(0)
+        copy_raw(3, 2)
         data_interleave(1)
         code_quantize(1, 2, OLD_PASSES)
+        grouped_of(3, "handover", 1)
+        scale_raw(3, 2)
         for h in range(HALVES):
             stage1(1, h, 2, OLD_PASSES)
         scale_out(2, 1, 3)
-        scale_out(3, 2, OLD_PASSES)
+        scale_out(3, 0, 1)
         code_quantize(2, 0, OLD_PASSES)
         transposes((0, NEW_PASS), (1, NEW_PASS))
         transposes((2, NEW_PASS), (3, NEW_PASS))
-        scale_out(3, 0, 2)
+        scale_out(3, 1, 2)
         stage1(2, 0, 0, OLD_PASSES)
         stage1(2, 1, 0, OLD_PASSES)
         for tile in range(4):

@@ -25,6 +25,7 @@ FP4_BYTES = 2
 
 SCALE_ROWS = 16
 QUADRANT = 32
+QUADRANTS = P // QUADRANT
 BANKS = 8
 
 TILES = M // P
@@ -90,6 +91,7 @@ def tile_coded_worker_products_s3_kernel(
             old_bytes.append(ob)
             new_code.append(nw)
             mask_tiles.append(mk)
+        new_blocks = {}
         data_raw = []
         for h in range(HALVES):
             dr = keep.tile([P, PACK, NH], BF16, name=f"data_raw_{h}")
@@ -106,8 +108,15 @@ def tile_coded_worker_products_s3_kernel(
         def load_old(j, i0=0, i1=2):
             nc.sync.dma_start(out=old_bytes[j][:, i0:i1, :], in_=old_rows[j, :, i0:i1, :])
 
-        def load_new(j):
-            nc.sync.dma_start(out=new_code[j][:], in_=new_rows[j].rearrange("p i k -> p (i k)"))
+        def load_new(j, tiles=2):
+            nc.sync.dma_start(out=new_code[j][:, : tiles * K1], in_=new_rows[j, :, :tiles, :].rearrange("p i k -> p (i k)"))
+
+        def load_new_blocks(tile):
+            blocks = keep.tile([P, QUADRANTS, P], BF16, name=f"new_blocks_{tile}", align_bytes=64)
+            new_blocks[tile] = blocks
+            rows = new_rows[tile // 2, :, tile % 2, :].rearrange("(b i) k -> i b k", i=QUADRANT)
+            for q in range(QUADRANTS):
+                nc.sync.dma_start(out=blocks[QUADRANT * q : QUADRANT * (q + 1)], in_=rows[:, :, P * q : P * (q + 1)])
 
         def load_mask(j):
             nc.sync.dma_start(out=mask_tiles[j][:], in_=mask_rows[j])
@@ -216,6 +225,21 @@ def tile_coded_worker_products_s3_kernel(
             nc.scalar.copy(out=pm[:], in_=new_words(tile).rearrange("p (w u) -> p u w", u=2))
             permuted[tile, "new"] = pm
 
+        def permute_blocks(tile):
+            pm = work.tile([P, 2, QUADRANTS, QUADRANT], F32, name=f"permuted_blocks_{tile}", tag="permuted_blocks", bufs=2, align_bytes=64)
+            words = new_blocks[tile][:].rearrange("p b k -> p (b k)").bitcast(F32)
+            nc.scalar.copy(out=pm[:], in_=words.rearrange("p (b j u) -> p u b j", u=2, j=QUADRANT))
+            permuted[tile, "blocks"] = pm
+
+        def turn_blocks(tile):
+            tb = work.tile([P, 2, P], F32, name=f"turned_{tile}", tag="turned", bufs=2, align_bytes=64)
+            nc.vector.transpose(tb[:].rearrange("p u m -> p (u m)"), permuted[tile, "blocks"][:].rearrange("p u b j -> p (u b j)"))
+            permuted[tile, "turned"] = tb
+
+        def copy_turned(tile):
+            dst = grouped_of(tile)[:, K_PASS * NEW_PASS :].bitcast(F32)
+            nc.scalar.copy(out=dst.rearrange("p (m u) -> p m u", u=2), in_=permuted[tile, "turned"][:].rearrange("p u m -> p m u"))
+
         def widen(tile, g0, g1):
             pairs = permuted_old(tile)[:, :, P * g0 : P * g1].bitcast(BF16).rearrange("p u (w e) -> p w u e", e=2)
             source = old_bytes[tile // 2][:, tile % 2, K_PASS * g0 : K_PASS * g1].bitcast(FP8)
@@ -254,6 +278,10 @@ def tile_coded_worker_products_s3_kernel(
         def code_transposes(tile):
             transposes((tile, 0), (tile, 1))
             transposes((tile, 2), (tile, NEW_PASS))
+
+        def old_transposes(tile):
+            transposes((tile, 0), (tile, 1))
+            transposes((tile, 2))
 
         def grouped_of(tile, tag="grouped", bufs=4):
             if tile not in grouped:
@@ -358,11 +386,11 @@ def tile_coded_worker_products_s3_kernel(
             )
             give_bank(f"s1_{tile}_{h}")
 
-        def scale_features(engine, tile, h0, h1):
+        def scale_features(engine, tile, h0, h1, parts=1):
             if tile not in coded:
                 c = work.tile([P, 2, F // PACK, 2], BF16, name=f"coded_{tile}", tag="coded", bufs=5, align_bytes=64)
                 coded[tile] = c
-            w = slice(P * h0, P * h1)
+            w = slice(P * h0 // parts, P * h1 // parts)
             engine.tensor_tensor(
                 out=coded[tile][:, :, w, :],
                 in0=masked[tile][:].rearrange("p (w u e) -> p u w e", u=2, e=2)[:, :, w, :],
@@ -388,6 +416,27 @@ def tile_coded_worker_products_s3_kernel(
             copy(out=cg[:].bitcast(F32), in_=coded_banks[tile][:].rearrange("p g u m -> p g m u"))
             coded_grouped[tile] = cg
             give_bank(f"cc_{tile}")
+
+        def coded_by_pass(tile):
+            cg = work.tile([P, X_PASSES, P, PACK], BF16, name=f"coded_grouped_{tile}", tag="coded_grouped", bufs=3, align_bytes=64)
+            codes = work.tile([P, X_PASSES, P], U32, name=f"coded_codes_{tile}", tag="coded_codes", bufs=3, align_bytes=256)
+            scales = work.tile([P, X_PASSES, P], U8, name=f"coded_scales_{tile}", tag="coded_scales", bufs=3, align_bytes=256)
+            words = coded[tile][:].rearrange("p u w e -> p (u w e)").bitcast(F32)
+            banks = []
+            for g in range(X_PASSES):
+                bank = take_bank(f"cc_{tile}_{g}", [P, 2, P])
+                banks.append(bank)
+                for u in range(2):
+                    first = (X_PASSES * u + g) * P
+                    nc.tensor.transpose(bank[:, u, :], words[:, first : first + P], ident[:])
+            for g in range(X_PASSES):
+                vector_copy(out=cg[:, g].bitcast(F32), in_=banks[g][:].rearrange("p u m -> p m u"))
+                give_bank(f"cc_{tile}_{g}")
+            for g in range(X_PASSES):
+                nc.vector.quantize_mx(
+                    out=codes[:, g, :].bitcast(FP8X4), scales=scales[:, g, :], in_=cg[:, g].rearrange("p m t -> p (m t)")
+                )
+            coded_ops[tile] = (codes, scales)
 
         def coded_quantize(tile):
             codes = work.tile([P, X_PASSES, P], U32, name=f"coded_codes_{tile}", tag="coded_codes", bufs=3, align_bytes=256)
@@ -451,8 +500,8 @@ def tile_coded_worker_products_s3_kernel(
                 emit_block(tile, b)
                 emit_block(tile, b + 1)
 
-        def stage2(tile, copies=(scalar_copy,), blocks=2):
-            for b in range(X_BLOCKS):
+        def stage2(tile, copies=(scalar_copy,), blocks=2, b0=0, b1=X_BLOCKS):
+            for b in range(b0, b1):
                 stage2_block(tile, b)
                 emit_block(tile, b, copies[b % len(copies)], blocks)
 
@@ -477,9 +526,10 @@ def tile_coded_worker_products_s3_kernel(
         load_scales(x_plane, x_scales)
         for g in range(X_PASSES):
             load_x_code(g)
-        load_new(3)
+        load_new(3, 1)
         load_mask(2)
         load_mask(3)
+        load_new_blocks(7)
 
         widen(0, 0, 1)
         widen(0, 1, OLD_PASSES)
@@ -571,20 +621,21 @@ def tile_coded_worker_products_s3_kernel(
         coded_quantize(0)
         scale_out(5)
         stage1(4, 1)
-        finish(3, 0)
+        add_mask(3, 0)
         code_quantize(5)
         for b in range(0, X_BLOCKS, 2):
             stage2_pair(0, b)
         for b in range(X_BLOCKS - 1):
             emit_block(0, b)
+        for quarter in range(2):
+            scale_features(nc.gpsimd, 3, quarter, quarter + 1, parts=2)
         finish(3, 1)
-        finish(4, 0)
+        add_mask(4, 0)
 
         turn_coded(1)
         emit_block(0, X_BLOCKS - 1)
         code_transposes(6)
         copy_new(6)
-        permute_new(7)
         cast(7)
         permute(7)
         coded_quantize(1)
@@ -597,40 +648,59 @@ def tile_coded_worker_products_s3_kernel(
         emit_block(1, 0)
         emit_block(1, 1)
 
-        turn_coded(2)
-        transposes((7, 0), (7, 1))
+        coded_transposes(2)
+        coded_transposes(3)
         emit_block(1, 2)
+        coded_copy(2)
         emit_block(1, 3)
-        transposes((7, 2), (7, NEW_PASS))
-        finish(5, 0)
-        finish(5, 1)
-        copy_new(7)
+        coded_copy(3)
+        permute_blocks(7)
+        add_mask(5, 0)
+        scale_features(nc.vector, 4, 0, 1)
         coded_quantize(2)
-        scale_out(7)
-        for h in range(HALVES):
-            stage1(6, h)
-
-        turn_coded(3)
-        turn_coded(4)
+        finish(5, 1)
+        scale_features(nc.gpsimd, 5, 0, 1)
+        stage1_paired(6)
         add_mask(6, 0)
         coded_quantize(3)
         add_mask(6, 1)
-        stage2_paired(2)
-        code_quantize(7)
+        for b in range(0, X_BLOCKS, 2):
+            stage2_pair(2, b)
+        emit_block(2, 0)
+        emit_block(2, 1)
+        coded_transposes(4)
+        old_transposes(7)
+        emit_block(2, 2)
+        coded_copy(4)
+        emit_block(2, 3)
+        scale_out(7, 0, 1)
         coded_quantize(4)
+        turn_blocks(7)
+        scale_out(7, 1, 2)
         scale_features(nc.vector, 6, 0, HALVES)
         stage2_paired(3)
-        stage1(7, 0)
-        finish(7, 0, nc.vector)
-        turn_coded(5)
-        turn_coded(6)
-        stage2_paired(4)
+        copy_turned(7)
+        scale_out(7, 2, OLD_PASSES)
+        code_quantize(7)
+        stage2_pair(4, 0)
+        emit_block(4, 0)
+        emit_block(4, 1)
+        turn_coded(5, vector_copy)
+        coded_transposes(6)
+        stage2_pair(4, 2)
+        emit_block(4, 2)
+        emit_block(4, 3)
+        coded_copy(6)
         coded_quantize(5)
+        stage1(7, 0)
+        add_mask(7, 0)
         coded_quantize(6)
+        scale_features(nc.vector, 7, 0, 1)
+        stage2(5, blocks=1, b1=2)
         stage1(7, 1)
         finish(7, 1, nc.vector)
-        stage2(5, blocks=1)
-        turn_coded(7, vector_copy)
-        coded_quantize(7)
-        stage2(6, (scalar_copy, vector_copy), blocks=1)
+        stage2(5, blocks=1, b0=2)
+        stage2(6, blocks=1, b1=2)
+        coded_by_pass(7)
+        stage2(6, blocks=1, b0=2)
         stage2(7, (scalar_copy, vector_copy), blocks=1)

from contextlib import ExitStack

import concourse.mybir as mybir
from concourse.masks import make_identity

M, K1, K2, F, B = 1024, 512, 1536, 1024, 2048
FLOPS = 2 * M * (K1 + K2) * F + 2 * M * F * B

F32 = mybir.dt.float32
BF16 = mybir.dt.bfloat16
I32 = mybir.dt.int32
U32 = mybir.dt.uint32
U8 = mybir.dt.uint8
FP8 = mybir.dt.float8_e4m3fn
FP8X4 = mybir.dt.float8_e4m3fn_x4
FP4X4 = mybir.dt.float4_e2m1fn_x4
ADD = mybir.AluOpType.add
MULT = mybir.AluOpType.mult

P = 128
PACK = 4
K_PASS = P * PACK
NH = 512
FP4_BYTES = 2

SCALE_ROWS = 16
QUADRANT = 32
QUADRANTS = P // QUADRANT
BANKS = 8

TILES = M // P
PAIRS = TILES // 2
HALVES = F // NH
OLD_PASSES = K2 // K_PASS
PASSES = OLD_PASSES + 1
NEW_PASS = OLD_PASSES
X_PASSES = F // K_PASS
X_BLOCKS = B // NH


def tile_coded_worker_products_s3_kernel(
    tc, code_new, data_new, code_old_bytes, code_old_scale, old_words, old_scales, mask, feature_scale, x_words, x_scales, out
):
    nc = tc.nc
    scalar_copy, vector_copy = nc.scalar.copy, nc.vector.tensor_copy

    with ExitStack() as ctx:
        keep = ctx.enter_context(tc.tile_pool(name="keep", bufs=1))
        work = ctx.enter_context(tc.tile_pool(name="work", bufs=3))
        psum = ctx.enter_context(tc.psum_pool(name="psum", bufs=1))
        ctx.enter_context(tc.manual_schedule())

        free_banks = list(range(BANKS))
        held = {}

        def take_bank(key, shape):
            b = free_banks.pop(0)
            held[key] = b
            bank = psum.tile(shape, F32, name=f"psum_{key}", tag=f"bank_{b}", bufs=1)
            return bank

        def give_bank(key):
            free_banks.append(held[key])

        old_plane = keep.tile([P, OLD_PASSES, F], U8, name="old_plane", align_bytes=256)
        x_plane = keep.tile([P, X_PASSES, B], U8, name="x_plane", align_bytes=256)
        warm = keep.tile([P, NH], BF16, name="warm")
        nc.vector.memset(warm[:].bitcast(I32), 0)
        ones = keep.tile([P, 1], F32, name="ones")
        nc.vector.memset(ones[:], 1.0)
        nc.vector.memset(old_plane[:].rearrange("p g n -> p (g n)").bitcast(I32), 0)
        nc.vector.memset(x_plane[:].rearrange("p g n -> p (g n)").bitcast(I32), 0)

        scale_cols = keep.tile([P, OLD_PASSES, PACK], F32, name="scale_cols")
        feature_cols = keep.tile([P, 2 * PACK], BF16, name="feature_cols")
        ident = keep.tile([P, P], F32, name="ident")
        make_identity(nc, ident[:])

        old_rows = code_old_bytes.rearrange("(j p i) k -> j p i k", p=P, i=2)
        new_rows = code_new.rearrange("(j p i) k -> j p i k", p=P, i=2)
        mask_rows = mask.rearrange("(j p i) f -> j p i f", p=P, i=2)
        out_rows = out.rearrange("(j p i) b -> j i p b", p=P, i=2)

        old_bytes = []
        new_code = []
        mask_tiles = []
        for j in range(PAIRS):
            ob = keep.tile([P, 2, K2], U8, name=f"old_bytes_{j}")
            nw = keep.tile([P, 2 * K1], BF16, name=f"new_code_{j}", align_bytes=64)
            mk = keep.tile([P, 2, F], BF16, name=f"mask_{j}")
            old_bytes.append(ob)
            new_code.append(nw)
            mask_tiles.append(mk)
        new_blocks = {}
        data_raw = []
        for h in range(HALVES):
            dr = keep.tile([P, PACK, NH], BF16, name=f"data_raw_{h}")
            data_raw.append(dr)
        old_code = []
        for g in range(OLD_PASSES):
            oc = keep.tile([P, FP4_BYTES * F], U8, name=f"old_code_{g}", align_bytes=256)
            old_code.append(oc)
        x_code = []
        for g in range(X_PASSES):
            xc = keep.tile([P, FP4_BYTES * B], U8, name=f"x_code_{g}", align_bytes=256)
            x_code.append(xc)

        def load_old(j, i0=0, i1=2):
            nc.sync.dma_start(out=old_bytes[j][:, i0:i1, :], in_=old_rows[j, :, i0:i1, :])

        def load_new(j, tiles=2):
            nc.sync.dma_start(out=new_code[j][:, : tiles * K1], in_=new_rows[j, :, :tiles, :].rearrange("p i k -> p (i k)"))

        def load_new_blocks(tile):
            blocks = keep.tile([P, QUADRANTS, P], BF16, name=f"new_blocks_{tile}", align_bytes=64)
            new_blocks[tile] = blocks
            rows = new_rows[tile // 2, :, tile % 2, :].rearrange("(b i) k -> i b k", i=QUADRANT)
            for q in range(QUADRANTS):
                nc.sync.dma_start(out=blocks[QUADRANT * q : QUADRANT * (q + 1)], in_=rows[:, :, P * q : P * (q + 1)])

        def load_mask(j):
            nc.sync.dma_start(out=mask_tiles[j][:], in_=mask_rows[j])

        def load_data(h):
            rows = data_new.rearrange("(p t) f -> p t f", t=PACK)
            nc.sync.dma_start(out=data_raw[h][:], in_=rows[:, :, NH * h : NH * (h + 1)])

        def load_old_code(g):
            nc.sync.dma_start(out=old_code[g][:], in_=old_words[g])

        def load_x_code(g):
            nc.sync.dma_start(out=x_code[g][:], in_=x_words[g])

        def load_scales(plane, source):
            for r in range(PACK):
                nc.sync.dma_start(
                    out=plane[r:P:QUADRANT, :, :].bitcast(I32),
                    in_=source.rearrange("g q n -> q g n")[r:SCALE_ROWS:PACK, :, :].bitcast(I32),
                )

        feature_all = keep.tile([P, 2, F // PACK, 2], BF16, name="feature_all")

        def spread_features():
            bank = take_bank("spread", [P, PACK, P])
            words = feature_cols[:].bitcast(F32)
            for c in range(PACK):
                nc.tensor.transpose(bank[:, c, :], words[:, c : c + 1].to_broadcast([P, P]), ident[:])
            return bank

        def copy_features(bank):
            dst = feature_all[:].rearrange("p u w e -> p (u w e)").bitcast(F32)
            nc.scalar.copy(
                out=dst.rearrange("p (u n c) -> p u n c", u=2, c=2), in_=bank[:].rearrange("p (c u) n -> p u n c", u=2)
            )
            give_bank("spread")

        def warm_up(count):
            bank = take_bank("warm", [P, NH])
            for n in range(count):
                nc.tensor.matmul(bank[:], lhsT=warm[:, 0:P], rhs=warm[:], start=True, stop=True)
            give_bank("warm")

        data_grouped = []
        data_codes = []
        data_scales = []
        for h in range(HALVES):
            dg = keep.tile([P, NH, PACK], BF16, name=f"data_grouped_{h}", align_bytes=64)
            dc = keep.tile([P, NH], U32, name=f"data_codes_{h}", align_bytes=256)
            ds = keep.tile([P, NH], U8, name=f"data_scales_{h}", align_bytes=256)
            data_grouped.append(dg)
            data_codes.append(dc)
            data_scales.append(ds)

        def data_interleave(h):
            nc.scalar.copy(
                out=data_grouped[h][:].rearrange("p (c i) t -> p c t i", i=PACK),
                in_=data_raw[h][:].rearrange("p t (c i) -> p c t i", i=PACK),
            )

        def data_quantize(h):
            nc.vector.quantize_mx(
                out=data_codes[h][:].bitcast(FP8X4),
                scales=data_scales[h][:],
                in_=data_grouped[h][:].rearrange("p n t -> p (n t)"),
            )

        old_rows_bf = {}
        permuted = {}
        parts = {}
        raws = {}
        in_order = set()
        grouped = {}
        code_ops = {}
        sums = {}
        masked = {}
        coded = {}
        coded_banks = {}
        coded_grouped = {}
        coded_ops = {}
        results = {}
        outs = {}

        def cast(tile):
            ob = work.tile([P, K2], BF16, name=f"old_bf_{tile}", tag="old_bf", bufs=3, align_bytes=64)
            old_rows_bf[tile] = ob
            nc.scalar.copy(out=ob[:], in_=old_bytes[tile // 2][:, tile % 2, :].bitcast(FP8))

        def new_words(tile):
            return new_code[tile // 2][:, K1 * (tile % 2) : K1 * (tile % 2 + 1)].bitcast(F32)

        def permuted_old(tile):
            if (tile, "old") not in permuted:
                pm = work.tile([P, 2, OLD_PASSES * P], F32, name=f"permuted_{tile}", tag="permuted", bufs=3)
                permuted[tile, "old"] = pm
            return permuted[tile, "old"]

        def permute(tile, g0=0, g1=OLD_PASSES):
            words = old_rows_bf[tile][:, K_PASS * g0 : K_PASS * g1].bitcast(F32)
            nc.scalar.copy(out=permuted_old(tile)[:, :, P * g0 : P * g1], in_=words.rearrange("p (w u) -> p u w", u=2))
            for g in range(g0, g1):
                in_order.add((tile, g))

        def permute_new(tile):
            pm = work.tile([P, 2, P], F32, name=f"permuted_new_{tile}", tag="permuted_new", bufs=3)
            nc.scalar.copy(out=pm[:], in_=new_words(tile).rearrange("p (w u) -> p u w", u=2))
            permuted[tile, "new"] = pm

        def permute_blocks(tile):
            pm = work.tile([P, 2, QUADRANTS, QUADRANT], F32, name=f"permuted_blocks_{tile}", tag="permuted_blocks", bufs=2, align_bytes=64)
            words = new_blocks[tile][:].rearrange("p b k -> p (b k)").bitcast(F32)
            nc.scalar.copy(out=pm[:], in_=words.rearrange("p (b j u) -> p u b j", u=2, j=QUADRANT))
            permuted[tile, "blocks"] = pm

        def turn_blocks(tile):
            tb = work.tile([P, 2, P], F32, name=f"turned_{tile}", tag="turned", bufs=2, align_bytes=64)
            nc.vector.transpose(tb[:].rearrange("p u m -> p (u m)"), permuted[tile, "blocks"][:].rearrange("p u b j -> p (u b j)"))
            permuted[tile, "turned"] = tb

        def copy_turned(tile):
            dst = grouped_of(tile)[:, K_PASS * NEW_PASS :].bitcast(F32)
            nc.scalar.copy(out=dst.rearrange("p (m u) -> p m u", u=2), in_=permuted[tile, "turned"][:].rearrange("p u m -> p m u"))

        def widen(tile, g0, g1):
            pairs = permuted_old(tile)[:, :, P * g0 : P * g1].bitcast(BF16).rearrange("p u (w e) -> p w u e", e=2)
            source = old_bytes[tile // 2][:, tile % 2, K_PASS * g0 : K_PASS * g1].bitcast(FP8)
            nc.vector.tensor_scalar(
                out=pairs, in0=source.rearrange("p (w u e) -> p w u e", u=2, e=2), scalar1=ones[:], scalar2=None, op0=MULT
            )
            for g in range(g0, g1):
                in_order.add((tile, g))

        def words_of(tile, g, u):
            if g == NEW_PASS:
                if (tile, "new") in permuted:
                    return permuted[tile, "new"][:, u, :]
                return new_words(tile)[:, u : 2 * P : 2]
            if (tile, g) in in_order:
                return permuted[tile, "old"][:, u, P * g : P * (g + 1)]
            return old_rows_bf[tile][:].bitcast(F32)[:, 2 * P * g + u : 2 * P * (g + 1) : 2]

        code_banks = {}
        unread = {}

        def slot_read(key):
            unread[key] = unread[key] - 1
            if unread[key] == 0:
                give_bank(key)

        def transposes(*slots):
            key = f"cb_{slots[0][0]}_{slots[0][1]}"
            bank = take_bank(key, [P, 2, 2, P])
            unread[key] = len(slots)
            for s, (tile, g) in enumerate(slots):
                for u in range(2):
                    nc.tensor.transpose(bank[:, s, u, :], words_of(tile, g, u), ident[:])
                code_banks[tile, g] = (bank, s, key)

        def code_transposes(tile):
            transposes((tile, 0), (tile, 1))
            transposes((tile, 2), (tile, NEW_PASS))

        def old_transposes(tile):
            transposes((tile, 0), (tile, 1))
            transposes((tile, 2))

        def grouped_of(tile, tag="grouped", bufs=4):
            if tile not in grouped:
                gr = work.tile([P, PASSES * P * PACK], BF16, name=f"grouped_{tile}", tag=tag, bufs=bufs, align_bytes=64)
                grouped[tile] = gr
            return grouped[tile]

        def passes_of(tile, g0, g1):
            if (tile, g0) in parts:
                part, first = parts[tile, g0]
                return part[:, K_PASS * (g0 - first) : K_PASS * (g1 - first)]
            return grouped_of(tile)[:, K_PASS * g0 : K_PASS * g1]

        def own_buffer(tile, g0, g1, tag):
            part = work.tile([P, K_PASS * (g1 - g0)], BF16, name=f"part_{tile}_{g0}", tag=tag, bufs=1, align_bytes=64)
            for g in range(g0, g1):
                parts[tile, g] = (part, g0)

        def copy_raw(tile, g):
            bank, s, key = code_banks[tile, g]
            raw = work.tile([P, K_PASS], BF16, name=f"raw_{tile}_{g}", tag="raw", bufs=2)
            raws[tile, g] = raw
            nc.scalar.copy(
                out=raw[:].bitcast(F32).rearrange("p (s m u) -> p s m u", m=P, u=2),
                in_=bank[:, s : s + 1].rearrange("p s u m -> p s m u"),
            )
            slot_read(key)

        def scale_raw(tile, g):
            nc.gpsimd.tensor_tensor(
                out=passes_of(tile, g, g + 1).rearrange("p (m t) -> p m t", t=PACK),
                in0=raws[tile, g][:].rearrange("p (m t) -> p m t", t=PACK),
                in1=scale_cols[:, g, :].unsqueeze(1).to_broadcast([P, P, PACK]),
                op=MULT,
            )

        def copy_new(tile):
            bank, s, key = code_banks[tile, NEW_PASS]
            dst = grouped_of(tile)[:, K_PASS * NEW_PASS :].bitcast(F32)
            nc.scalar.copy(
                out=dst.rearrange("p (s m u) -> p s m u", m=P, u=2), in_=bank[:, s : s + 1].rearrange("p s u m -> p s m u")
            )
            slot_read(key)

        def scale_out(tile, g0=0, g1=OLD_PASSES):
            for g in range(g0, g1):
                bank, s, key = code_banks[tile, g]
                nc.vector.tensor_tensor(
                    out=passes_of(tile, g, g + 1).rearrange("p (m u e) -> p m u e", u=2, e=2),
                    in0=bank[:, s].bitcast(BF16).rearrange("p u (m e) -> p m u e", e=2),
                    in1=scale_cols[:, g, :].rearrange("p (u e) -> p u e", e=2).unsqueeze(1).to_broadcast([P, P, 2, 2]),
                    op=MULT,
                )
                slot_read(key)

        def code_quantize(tile, g0=0, g1=PASSES):
            if tile not in code_ops:
                codes = work.tile([P, PASSES * P], U32, name=f"code_codes_{tile}", tag="code_codes", bufs=4, align_bytes=256)
                scales = work.tile([P, PASSES * P], U8, name=f"code_scales_{tile}", tag="code_scales", bufs=4, align_bytes=256)
                code_ops[tile] = (codes, scales)
            codes, scales = code_ops[tile]
            nc.vector.quantize_mx(
                out=codes[:, P * g0 : P * g1].bitcast(FP8X4),
                scales=scales[:, P * g0 : P * g1],
                in_=passes_of(tile, g0, g1),
            )

        def stage1(tile, h, g0=0, g1=PASSES):
            codes, scales = code_ops[tile]
            for g in range(g0, g1):
                if g == 0:
                    acc = take_bank(f"s1_{tile}_{h}", [P, NH])
                    sums[tile, h] = acc
                if g == NEW_PASS:
                    rhs = data_codes[h][:].bitcast(FP8X4)
                    rhs_scale = data_scales[h][:]
                else:
                    rhs = old_code[g][:, FP4_BYTES * NH * h : FP4_BYTES * NH * (h + 1)].bitcast(FP4X4)
                    rhs_scale = old_plane[:, g, NH * h : NH * (h + 1)]
                nc.tensor.matmul_mx(
                    out=sums[tile, h][:],
                    lhsT=codes[:, P * g : P * (g + 1)].bitcast(FP8X4),
                    lhsT_scale=scales[:, P * g : P * (g + 1)],
                    rhs=rhs,
                    rhs_scale=rhs_scale,
                    start=(g == 0),
                    stop=(g == NEW_PASS),
                )

        def stage1_paired(tile, passes=PASSES):
            for g in range(passes):
                for h in range(HALVES):
                    stage1(tile, h, g, g + 1)

        def add_mask(tile, h):
            if tile not in masked:
                mt = work.tile([P, F], F32, name=f"masked_{tile}", tag="masked", bufs=4)
                masked[tile] = mt
            cols = slice(NH * h, NH * (h + 1))
            nc.vector.tensor_tensor(
                out=masked[tile][:, cols], in0=sums[tile, h][:], in1=mask_tiles[tile // 2][:, tile % 2, cols], op=ADD
            )
            give_bank(f"s1_{tile}_{h}")

        def scale_features(engine, tile, h0, h1, parts=1):
            if tile not in coded:
                c = work.tile([P, 2, F // PACK, 2], BF16, name=f"coded_{tile}", tag="coded", bufs=5, align_bytes=64)
                coded[tile] = c
            w = slice(P * h0 // parts, P * h1 // parts)
            engine.tensor_tensor(
                out=coded[tile][:, :, w, :],
                in0=masked[tile][:].rearrange("p (w u e) -> p u w e", u=2, e=2)[:, :, w, :],
                in1=feature_all[:, :, w, :],
                op=MULT,
            )

        def finish(tile, h, engine=nc.gpsimd):
            add_mask(tile, h)
            scale_features(engine, tile, h, h + 1)

        def coded_transposes(tile):
            bank = take_bank(f"cc_{tile}", [P, X_PASSES, 2, P])
            words = coded[tile][:].rearrange("p u w e -> p (u w e)").bitcast(F32)
            for g in range(X_PASSES):
                for u in range(2):
                    first = (X_PASSES * u + g) * P
                    nc.tensor.transpose(bank[:, g, u, :], words[:, first : first + P], ident[:])
            coded_banks[tile] = bank

        def coded_copy(tile, copy=scalar_copy):
            cg = work.tile([P, X_PASSES, P, PACK], BF16, name=f"coded_grouped_{tile}", tag="coded_grouped", bufs=3, align_bytes=64)
            copy(out=cg[:].bitcast(F32), in_=coded_banks[tile][:].rearrange("p g u m -> p g m u"))
            coded_grouped[tile] = cg
            give_bank(f"cc_{tile}")

        def coded_by_pass(tile):
            cg = work.tile([P, X_PASSES, P, PACK], BF16, name=f"coded_grouped_{tile}", tag="coded_grouped", bufs=3, align_bytes=64)
            codes = work.tile([P, X_PASSES, P], U32, name=f"coded_codes_{tile}", tag="coded_codes", bufs=3, align_bytes=256)
            scales = work.tile([P, X_PASSES, P], U8, name=f"coded_scales_{tile}", tag="coded_scales", bufs=3, align_bytes=256)
            words = coded[tile][:].rearrange("p u w e -> p (u w e)").bitcast(F32)
            banks = []
            for g in range(X_PASSES):
                bank = take_bank(f"cc_{tile}_{g}", [P, 2, P])
                banks.append(bank)
                for u in range(2):
                    first = (X_PASSES * u + g) * P
                    nc.tensor.transpose(bank[:, u, :], words[:, first : first + P], ident[:])
            for g in range(X_PASSES):
                vector_copy(out=cg[:, g].bitcast(F32), in_=banks[g][:].rearrange("p u m -> p m u"))
                give_bank(f"cc_{tile}_{g}")
            for g in range(X_PASSES):
                nc.vector.quantize_mx(
                    out=codes[:, g, :].bitcast(FP8X4), scales=scales[:, g, :], in_=cg[:, g].rearrange("p m t -> p (m t)")
                )
            coded_ops[tile] = (codes, scales)

        def coded_quantize(tile):
            codes = work.tile([P, X_PASSES, P], U32, name=f"coded_codes_{tile}", tag="coded_codes", bufs=3, align_bytes=256)
            scales = work.tile([P, X_PASSES, P], U8, name=f"coded_scales_{tile}", tag="coded_scales", bufs=3, align_bytes=256)
            nc.vector.quantize_mx(
                out=codes[:].rearrange("p g m -> p (g m)").bitcast(FP8X4),
                scales=scales[:].rearrange("p g m -> p (g m)"),
                in_=coded_grouped[tile][:].rearrange("p g m t -> p (g m t)"),
            )
            coded_ops[tile] = (codes, scales)

        def turn_coded(tile, copy=scalar_copy):
            coded_transposes(tile)
            coded_copy(tile, copy)

        def stage2_block(tile, b):
            codes, scales = coded_ops[tile]
            acc = take_bank(f"s2_{tile}_{b}", [P, NH])
            for g in range(X_PASSES):
                nc.tensor.matmul_mx(
                    out=acc[:],
                    lhsT=codes[:, g, :].bitcast(FP8X4),
                    lhsT_scale=scales[:, g, :],
                    rhs=x_code[g][:, FP4_BYTES * NH * b : FP4_BYTES * NH * (b + 1)].bitcast(FP4X4),
                    rhs_scale=x_plane[:, g, NH * b : NH * (b + 1)],
                    start=(g == 0),
                    stop=(g == X_PASSES - 1),
                )
            outs[tile, b] = acc

        def stage2_pair(tile, b):
            codes, scales = coded_ops[tile]
            for c in (b, b + 1):
                acc = take_bank(f"s2_{tile}_{c}", [P, NH])
                outs[tile, c] = acc
            for g in range(X_PASSES):
                for c in (b, b + 1):
                    nc.tensor.matmul_mx(
                        out=outs[tile, c][:],
                        lhsT=codes[:, g, :].bitcast(FP8X4),
                        lhsT_scale=scales[:, g, :],
                        rhs=x_code[g][:, FP4_BYTES * NH * c : FP4_BYTES * NH * (c + 1)].bitcast(FP4X4),
                        rhs_scale=x_plane[:, g, NH * c : NH * (c + 1)],
                        start=(g == 0),
                        stop=(g == X_PASSES - 1),
                    )

        def emit_block(tile, b, copy=scalar_copy, blocks=2):
            if tile not in results:
                rs = work.tile([P, B], F32, name=f"result_{tile}", tag="result", bufs=3)
                results[tile] = rs
            copy(out=results[tile][:, NH * b : NH * (b + 1)], in_=outs[tile, b][:])
            give_bank(f"s2_{tile}_{b}")
            if (b + 1) % blocks == 0:
                cols = slice(NH * (b + 1 - blocks), NH * (b + 1))
                nc.sync.dma_start(out=out_rows[tile // 2, tile % 2, :, cols], in_=results[tile][:, cols])

        def stage2_paired(tile):
            for b in range(0, X_BLOCKS, 2):
                stage2_pair(tile, b)
                emit_block(tile, b)
                emit_block(tile, b + 1)

        def stage2(tile, copies=(scalar_copy,), blocks=2, b0=0, b1=X_BLOCKS):
            for b in range(b0, b1):
                stage2_block(tile, b)
                emit_block(tile, b, copies[b % len(copies)], blocks)

        load_old(0, 0, 1)
        nc.scalar.dma_start(out=scale_cols[:], in_=code_old_scale.rearrange("o (g p c) -> p (o g) c", p=P, c=PACK))
        nc.scalar.dma_start(out=feature_cols[:], in_=feature_scale.rearrange("(p c) -> p c", p=P))
        load_old(0, 1, 2)
        load_old(1)
        load_old_code(0)
        load_scales(old_plane, old_scales)
        load_data(0)
        load_old_code(1)
        load_old_code(2)
        load_data(1)
        load_new(0)
        load_new(1)
        load_old(2)
        load_new(2)
        load_mask(0)
        load_old(3)
        load_mask(1)
        load_scales(x_plane, x_scales)
        for g in range(X_PASSES):
            load_x_code(g)
        load_new(3, 1)
        load_mask(2)
        load_mask(3)
        load_new_blocks(7)

        widen(0, 0, 1)
        widen(0, 1, OLD_PASSES)
        cast(1)
        warm_up(4)
        transposes((0, 0))
        spread = spread_features()
        cast(2)
        cast(3)
        transposes((0, 1), (0, 2))
        warm_up(2)
        scale_out(0, 0, 2)
        code_quantize(0, 0, 1)
        transposes((1, 0), (1, 1))
        scale_out(0, 2, OLD_PASSES)
        transposes((1, 2), (2, 0))
        for h in range(HALVES):
            stage1(0, h, 0, 1)
        scale_out(1, 0, 2)
        code_quantize(0, 1, OLD_PASSES)
        code_quantize(1, 0, 2)
        transposes((2, 1), (2, 2))
        copy_features(spread)
        transposes((3, 0), (3, 1))
        permute(3, 2, OLD_PASSES)
        transposes((3, 2))
        own_buffer(1, 2, OLD_PASSES, "handover")
        scale_out(1, 2, OLD_PASSES)
        scale_out(2, 0, 1)
        for tile, g in ((0, 1), (1, 0), (1, 1), (0, 2)):
            for h in range(HALVES):
                stage1(tile, h, g, g + 1)
        data_interleave(0)
        copy_raw(3, 2)
        data_interleave(1)
        code_quantize(1, 2, OLD_PASSES)
        grouped_of(3, "handover", 1)
        scale_raw(3, 2)
        for h in range(HALVES):
            stage1(1, h, 2, OLD_PASSES)
        scale_out(2, 1, 3)
        scale_out(3, 0, 1)
        code_quantize(2, 0, OLD_PASSES)
        transposes((0, NEW_PASS), (1, NEW_PASS))
        transposes((2, NEW_PASS), (3, NEW_PASS))
        scale_out(3, 1, 2)
        stage1(2, 0, 0, OLD_PASSES)
        stage1(2, 1, 0, OLD_PASSES)
        for tile in range(4):
            copy_new(tile)
        data_quantize(0)
        code_quantize(0, NEW_PASS, PASSES)
        code_quantize(1, NEW_PASS, PASSES)
        data_quantize(1)
        code_quantize(2, NEW_PASS, PASSES)
        code_quantize(3)
        cast(4)
        permute_new(4)
        permute(4, 0, 2)
        permute(4, 2, OLD_PASSES)
        cast(5)
        for h in range(HALVES):
            for tile in range(2):
                stage1(tile, h, NEW_PASS)
        for h in range(HALVES):
            stage1(2, h, NEW_PASS)
        finish(0, 0)
        add_mask(1, 0)
        finish(0, 1)
        code_transposes(4)
        copy_new(4)
        permute(5)
        permute_new(5)
        stage1_paired(3)
        scale_out(4)
        finish(1, 1)
        code_quantize(4)
        scale_features(nc.gpsimd, 1, 0, 1)

        turn_coded(0)
        cast(6)
        finish(2, 0)
        finish(2, 1)
        code_transposes(5)
        copy_new(5)
        permute_new(6)
        permute(6)
        stage1(4, 0)
        coded_quantize(0)
        scale_out(5)
        stage1(4, 1)
        add_mask(3, 0)
        code_quantize(5)
        for b in range(0, X_BLOCKS, 2):
            stage2_pair(0, b)
        for b in range(X_BLOCKS - 1):
            emit_block(0, b)
        for quarter in range(2):
            scale_features(nc.gpsimd, 3, quarter, quarter + 1, parts=2)
        finish(3, 1)
        add_mask(4, 0)

        turn_coded(1)
        emit_block(0, X_BLOCKS - 1)
        code_transposes(6)
        copy_new(6)
        cast(7)
        permute(7)
        coded_quantize(1)
        scale_out(6)
        finish(4, 1)
        code_quantize(6)
        stage1_paired(5)
        for b in range(0, X_BLOCKS, 2):
            stage2_pair(1, b)
        emit_block(1, 0)
        emit_block(1, 1)

        coded_transposes(2)
        coded_transposes(3)
        emit_block(1, 2)
        coded_copy(2)
        emit_block(1, 3)
        coded_copy(3)
        permute_blocks(7)
        add_mask(5, 0)
        scale_features(nc.vector, 4, 0, 1)
        coded_quantize(2)
        finish(5, 1)
        scale_features(nc.gpsimd, 5, 0, 1)
        stage1_paired(6)
        add_mask(6, 0)
        coded_quantize(3)
        add_mask(6, 1)
        for b in range(0, X_BLOCKS, 2):
            stage2_pair(2, b)
        emit_block(2, 0)
        emit_block(2, 1)
        coded_transposes(4)
        old_transposes(7)
        emit_block(2, 2)
        coded_copy(4)
        emit_block(2, 3)
        scale_out(7, 0, 1)
        coded_quantize(4)
        turn_blocks(7)
        scale_out(7, 1, 2)
        scale_features(nc.vector, 6, 0, HALVES)
        stage2_paired(3)
        copy_turned(7)
        scale_out(7, 2, OLD_PASSES)
        code_quantize(7)
        stage2_pair(4, 0)
        emit_block(4, 0)
        emit_block(4, 1)
        turn_coded(5, vector_copy)
        coded_transposes(6)
        stage2_pair(4, 2)
        emit_block(4, 2)
        emit_block(4, 3)
        coded_copy(6)
        coded_quantize(5)
        stage1(7, 0)
        add_mask(7, 0)
        coded_quantize(6)
        scale_features(nc.vector, 7, 0, 1)
        stage2(5, blocks=1, b1=2)
        stage1(7, 1)
        finish(7, 1, nc.vector)
        stage2(5, blocks=1, b0=2)
        stage2(6, blocks=1, b1=2)
        coded_by_pass(7)
        stage2(6, blocks=1, b0=2)
        stage2(7, (scalar_copy, vector_copy), blocks=1)
